import numpy as np
import ml_dtypes


def mxq(x, axis, fmt="e4m3"):
    dtype, down = {"e4m3": (ml_dtypes.float8_e4m3fn, 7), "e5m2": (ml_dtypes.float8_e5m2, 14)}[fmt]
    v = np.moveaxis(np.asarray(x, np.float32).astype(ml_dtypes.bfloat16).astype(np.float64), axis, -1)
    blocks = v.reshape(v.shape[:-1] + (-1, 32))
    amax = np.abs(blocks).max(-1, keepdims=True)
    byte = np.maximum(np.where(amax > 0, np.frexp(amax)[1] - 1 + 127, 0) - down, 1)
    scale = np.exp2(byte - 127.0)
    codes = (blocks / scale).astype(np.float32).astype(dtype).astype(np.float64)
    return np.moveaxis((codes * scale).reshape(v.shape), -1, axis)


WIDE = False


def mx_kscale(k):
    if not WIDE:
        return np.ones(k)
    levels = np.array([10, -10, 5, -5, 0])
    if k % 512:
        return np.exp2(np.random.permutation(np.resize(levels, k // 32))).repeat(32)
    a = np.empty((k // 512, 16))
    for p in range(k // 512):
        a[p, :8] = np.random.permutation(np.resize(levels, 8))
        for g in range(8):
            far = levels[np.abs(levels - a[p, g]) >= 10]
            a[p, g + 8] = far[np.random.randint(len(far))]
    return np.exp2(a.ravel()).repeat(32)


def f64(x):
    return np.asarray(x).astype(np.float64)


def striped(idx):
    return np.tile(idx.reshape(-1, 16).T, (8, 1)).astype(np.uint16)


def unstriped(offs):
    return offs[:16].T.reshape(-1).astype(np.int64)


E2M1 = np.array([0.0, 0.5, 1.0, 1.5, 2.0, 3.0, 4.0, 6.0, -0.0, -0.5, -1.0, -1.5, -2.0, -3.0, -4.0, -6.0])


def pack_fp4(w):
    k, n = w.shape
    w = f64(np.asarray(w, np.float32).astype(ml_dtypes.bfloat16)).reshape(k // 32, 32, n)
    amax = np.abs(w).max(1)
    mant, ex = np.frexp(amax / 6.0)
    byte = np.clip(np.where(amax > 0, np.where(mant > 0.5, ex, ex - 1) + 127, 1), 1, 254)
    scaled = (w * np.exp2(127.0 - byte)[:, None, :]).reshape(k, n).astype(np.float32)
    c = np.ascontiguousarray(scaled.reshape(k // 512, 128, 4, n).transpose(0, 1, 3, 2)).astype(ml_dtypes.float4_e2m1fn).view(np.uint8) & 0xF
    words = (c[..., 0::2] | (c[..., 1::2] << 4)).reshape(k // 512, 128, 2 * n)
    return np.ascontiguousarray(words), np.ascontiguousarray(byte.astype(np.uint8).reshape(k // 512, 16, n))


def unpack_fp4(words, scales):
    g, _, n = scales.shape
    words = np.ascontiguousarray(words).reshape(g, 128, n, 2)
    nib = np.empty((g, 128, n, 4), np.uint8)
    nib[..., 0::2] = words & 0xF
    nib[..., 1::2] = words >> 4
    vals = E2M1[nib] * np.repeat(np.exp2(scales.astype(np.float64) - 127.0), 8, axis=1)[..., None]
    return vals.transpose(0, 1, 3, 2).reshape(g * 512, n)


K, T, S, N, U = 512, 2048, 1024, 256, 2048
P = 2 ** 7


def setup_inputs():
    n = np.random.standard_normal
    s = mx_kscale(K)[:, None]
    packed_w1 = pack_fp4(n((K, N)) / np.sqrt(K) / s)
    return {
        "xT": (n((K, T)) * s).astype(np.float32),
        "mem": n((N, U)).astype(np.float32),
        "w1_words": packed_w1[0],
        "w1_scales": packed_w1[1],
        "old": np.tile(np.random.uniform(0.5, 0.95, S), (P, 1)).astype(np.float32),
        "new": np.tile(np.random.uniform(0.05, 0.5, S), (P, 1)).astype(np.float32),
        "offs": striped(np.random.permutation(T)[:S]),
        "slot": striped(np.random.permutation(U)[:S]),
    }


def reference(xT, mem, w1_words, w1_scales, old, new, offs, slot):
    xq = mxq(f64(xT)[:, unstriped(offs)], 0, "e4m3")
    y = np.tanh(unpack_fp4(w1_words, w1_scales).T @ xq)
    out = f64(mem).copy()
    out[:, unstriped(slot)] = f64(mem)[:, unstriped(slot)] * f64(old)[:1] + y * f64(new)[:1]
    return out

@@ -1,0 +1,130 @@
+from contextlib import ExitStack
+
+import concourse.mybir as mybir
+from concourse.masks import make_identity
+
+K, T, S, N, U = 512, 2048, 1024, 256, 2048
+FLOPS = 2 * K * S * N
+
+F32 = mybir.dt.float32
+BF16 = mybir.dt.bfloat16
+I32 = mybir.dt.int32
+U32 = mybir.dt.uint32
+U16 = mybir.dt.uint16
+U8 = mybir.dt.uint8
+FP8X4 = mybir.dt.float8_e4m3fn_x4
+FP4X4 = mybir.dt.float4_e2m1fn_x4
+COPY = mybir.ActivationFunctionType.Copy
+TANH = mybir.ActivationFunctionType.Tanh
+MULT = mybir.AluOpType.mult
+ADD = mybir.AluOpType.add
+
+P = 128
+HALF = S // 2
+CH = HALF // P
+LC = HALF // 16
+
+
+def tile_picked_ema_tanh_e_kernel(tc, xT, mem, w1_words, w1_scales, old, new, offs, slot, out):
+    nc = tc.nc
+    with ExitStack() as ctx:
+        keep = ctx.enter_context(tc.tile_pool(name="keep", bufs=1))
+        ypsum = ctx.enter_context(tc.psum_pool(name="ypsum", bufs=4))
+        tpsum = ctx.enter_context(tc.psum_pool(name="tpsum", bufs=4))
+
+        offs_sb = keep.tile([P, S // 16], U16, name="offs_sb")
+        slot_sb = keep.tile([P, S // 16], U16, name="slot_sb")
+        planes = [keep.tile([P, T], F32, name="plane%d" % j) for j in range(4)]
+        mems = [keep.tile([P, U], F32, name="mem%d" % b) for b in range(2)]
+        w_words = keep.tile([P, 2 * N], U8, name="w_words", align_bytes=64)
+        w_scales = keep.tile([P, N], U8, name="w_scales", align_bytes=64)
+        rows = keep.tile([P, P], F32, name="rows")
+        ident = keep.tile([P, P], F32, name="ident")
+
+        make_identity(nc, ident[:])
+        nc.vector.memset(rows[:], 0.0)
+        nc.vector.memset(w_scales[:].bitcast(I32), 0)
+        x_rows = xT.rearrange("(p j) t -> p j t", j=4)
+        nc.sync.dma_start(offs_sb[:], offs)
+        for j in range(4):
+            nc.sync.dma_start(planes[j][:], x_rows[:, j, :])
+        nc.scalar.dma_start(rows[0:8, :], old[0:1, :].rearrange("o (c n) -> (o c) n", n=P))
+        nc.scalar.dma_start(rows[8:16, :], new[0:1, :].rearrange("o (c n) -> (o c) n", n=P))
+        nc.sync.dma_start(slot_sb[:], slot)
+        nc.sync.dma_start(mems[0][:], mem[0:P, :])
+        nc.sync.dma_start(w_words[:].bitcast(I32), w1_words[0].bitcast(I32))
+        nc.sync.dma_start(mems[1][:], mem[P : 2 * P, :])
+        for q in range(4):
+            nc.gpsimd.dma_start(w_scales[32 * q : 32 * q + 4, :].bitcast(I32), w1_scales[0, 4 * q : 4 * q + 4, :].bitcast(I32))
+
+        colbank = tpsum.tile([P, CH, P], F32, name="tbank", tag="tbank")
+        nc.tensor.transpose(colbank[:, 0, :], rows[:], ident[:])
+        cols = keep.tile([P, 16], F32, name="cols")
+        nc.scalar.activation(cols[:], colbank[:, 0, 0:16], COPY)
+        old_sb = keep.tile([P, S], F32, name="old_sb")
+        for h in range(2):
+            oldbank = tpsum.tile([P, CH, P], F32, name="tbank", tag="tbank")
+            for c in range(CH):
+                i = CH * h + c
+                nc.tensor.transpose(oldbank[:, c, :], cols[:, i : i + 1].to_broadcast([P, P]), ident[:])
+            nc.scalar.copy(old_sb[:, h * HALF : (h + 1) * HALF], oldbank[:].rearrange("p c n -> p (c n)"))
+
+        g01 = keep.tile([P, 2, S], BF16, name="g01")
+        g23 = [keep.tile([P, 2, HALF], BF16, name="g23_%d" % h) for h in range(2)]
+        woven = [keep.tile([P, HALF, 4], BF16, name="woven%d" % h, align_bytes=64) for h in range(2)]
+        codes = [keep.tile([P, HALF], U32, name="codes%d" % h, align_bytes=64) for h in range(2)]
+        scales = [keep.tile([P, HALF], U8, name="scales%d" % h, align_bytes=64) for h in range(2)]
+        kept1 = keep.tile([P, S], F32, name="kept1")
+        kept0 = keep.tile([P, S], F32, name="kept0")
+        fresh0 = keep.tile([P, S], F32, name="fresh0")
+
+        for j in range(2):
+            nc.vector.tensor_copy(g01[:, j, :], planes[j][:].indirect(offs_sb[:]))
+        for h in range(2):
+            nc.scalar.copy(woven[h][:, :, 0:2], g01[:, :, h * HALF : (h + 1) * HALF].rearrange("p j n -> p n j"))
+        for j in range(2):
+            for h in range(2):
+                nc.vector.tensor_copy(g23[h][:, j, :], planes[2 + j][:].indirect(offs_sb[:, h * LC : (h + 1) * LC]))
+        for h in range(2):
+            nc.scalar.copy(woven[h][:, :, 2:4], g23[h][:].rearrange("p j n -> p n j"))
+
+        for h in range(2):
+            hs = slice(h * HALF, (h + 1) * HALF)
+            nc.vector.tensor_tensor(kept0[:, hs], mems[0][:].indirect(slot_sb[:, h * LC : (h + 1) * LC]), old_sb[:, hs], MULT)
+            nc.vector.quantize_mx(out=codes[h][:].bitcast(FP8X4), scales=scales[h][:], in_=woven[h][:].rearrange("p n j -> p (n j)"))
+        nc.vector.tensor_tensor(kept1[:], mems[1][:].indirect(slot_sb[:]), old_sb[:], MULT)
+
+        def fresh(b, h, dst):
+            ybank = ypsum.tile([P, CH, P], F32, name="ybank", tag="ybank")
+            for c in range(CH):
+                cs = slice(c * P, (c + 1) * P)
+                nc.tensor.matmul_mx(
+                    out=ybank[:, c, :],
+                    lhsT=codes[h][:, cs].bitcast(FP8X4),
+                    lhsT_scale=scales[h][:, cs],
+                    rhs=w_words[:, 2 * P * b : 2 * P * (b + 1)].bitcast(FP4X4),
+                    rhs_scale=w_scales[:, P * b : P * (b + 1)],
+                    start=True,
+                    stop=True,
+                )
+            y = keep.tile([P, CH, P], F32, name="y%d_%d" % (b, h))
+            nc.scalar.activation(y[:], ybank[:], TANH)
+            u = keep.tile([P, CH, P], F32, name="u%d_%d" % (b, h))
+            ubank = tpsum.tile([P, CH, P], F32, name="tbank", tag="tbank")
+            for c in range(CH):
+                i = 8 + CH * h + c
+                nc.scalar.activation(u[:, c, :], y[:, c, :], COPY, scale=cols[:, i : i + 1])
+            for c in range(CH):
+                nc.tensor.transpose(ubank[:, c, :], u[:, c, :], ident[:])
+            nc.scalar.copy(dst, ubank[:].rearrange("p c n -> p (c n)"))
+
+        for h in range(2):
+            hs = slice(h * HALF, (h + 1) * HALF)
+            fresh1 = keep.tile([P, HALF], F32, name="fresh1_%d" % h)
+            fresh(1, h, fresh1[:])
+            nc.vector.tensor_tensor(mems[1][:].indirect(slot_sb[:, h * LC : (h + 1) * LC]), kept1[:, hs], fresh1[:], ADD)
+        nc.sync.dma_start(out[P : 2 * P, :], mems[1][:])
+        for h in range(2):
+            fresh(0, h, fresh0[:, h * HALF : (h + 1) * HALF])
+        nc.vector.tensor_tensor(mems[0][:].indirect(slot_sb[:]), kept0[:], fresh0[:], ADD)
+        nc.sync.dma_start(out[0:P, :], mems[0][:])

@@ -38,61 +38,64 @@ def tile_picked_ema_tanh_e_kernel(tc, xT, mem, w1_words, w1_scales, old, new, of
         mems = [keep.tile([P, U], F32, name="mem%d" % b) for b in range(2)]
         w_words = keep.tile([P, 2 * N], U8, name="w_words", align_bytes=64)
         w_scales = keep.tile([P, N], U8, name="w_scales", align_bytes=64)
-        rows = keep.tile([P, P], F32, name="rows")
+        old_cols = [keep.tile([P, CH], F32, name="old_cols%d" % h, tag="stage%d" % h, align_bytes=64) for h in range(2)]
+        new_cols = keep.tile([P, 2, CH], F32, name="new_cols")
         ident = keep.tile([P, P], F32, name="ident")
 
+        nc.gpsimd.memset(w_scales[:].bitcast(I32), 0)
         make_identity(nc, ident[:])
-        nc.vector.memset(rows[:], 0.0)
-        nc.vector.memset(w_scales[:].bitcast(I32), 0)
         x_rows = xT.rearrange("(p j) t -> p j t", j=4)
+        for h in range(2):
+            nc.scalar.dma_start(old_cols[h][:], old[0:1, h * HALF : (h + 1) * HALF].rearrange("o (p c) -> (o p) c", c=CH))
+        nc.sync.dma_start(planes[0][:], x_rows[:, 0, :])
         nc.sync.dma_start(offs_sb[:], offs)
-        for j in range(4):
-            nc.sync.dma_start(planes[j][:], x_rows[:, j, :])
-        nc.scalar.dma_start(rows[0:8, :], old[0:1, :].rearrange("o (c n) -> (o c) n", n=P))
-        nc.scalar.dma_start(rows[8:16, :], new[0:1, :].rearrange("o (c n) -> (o c) n", n=P))
+        nc.sync.dma_start(planes[1][:], x_rows[:, 1, :])
+        nc.sync.dma_start(planes[2][:], x_rows[:, 2, :])
         nc.sync.dma_start(slot_sb[:], slot)
+        nc.sync.dma_start(planes[3][:], x_rows[:, 3, :])
         nc.sync.dma_start(mems[0][:], mem[0:P, :])
         nc.sync.dma_start(w_words[:].bitcast(I32), w1_words[0].bitcast(I32))
-        nc.sync.dma_start(mems[1][:], mem[P : 2 * P, :])
         for q in range(4):
-            nc.gpsimd.dma_start(w_scales[32 * q : 32 * q + 4, :].bitcast(I32), w1_scales[0, 4 * q : 4 * q + 4, :].bitcast(I32))
+            nc.sync.dma_start(w_scales[32 * q : 32 * q + 4, :].bitcast(I32), w1_scales[0, 4 * q : 4 * q + 4, :].bitcast(I32))
+        nc.sync.dma_start(mems[1][:], mem[P : 2 * P, :])
+        nc.sync.dma_start(new_cols[:], new[0:1, :].rearrange("o (h p c) -> (o p) h c", h=2, c=CH))
 
-        colbank = tpsum.tile([P, CH, P], F32, name="tbank", tag="tbank")
-        nc.tensor.transpose(colbank[:, 0, :], rows[:], ident[:])
-        cols = keep.tile([P, 16], F32, name="cols")
-        nc.scalar.activation(cols[:], colbank[:, 0, 0:16], COPY)
-        old_sb = keep.tile([P, S], F32, name="old_sb")
+        old1 = keep.tile([P, S], F32, name="old1")
+        old0 = [keep.tile([P, HALF], F32, name="old0_%d" % h, tag="late%d" % h, align_bytes=64) for h in range(2)]
         for h in range(2):
             oldbank = tpsum.tile([P, CH, P], F32, name="tbank", tag="tbank")
             for c in range(CH):
-                i = CH * h + c
-                nc.tensor.transpose(oldbank[:, c, :], cols[:, i : i + 1].to_broadcast([P, P]), ident[:])
-            nc.scalar.copy(old_sb[:, h * HALF : (h + 1) * HALF], oldbank[:].rearrange("p c n -> p (c n)"))
+                nc.tensor.transpose(oldbank[:, c, :], old_cols[h][:, c : c + 1].to_broadcast([P, P]), ident[:])
+            for dst in (old0[h][:], old1[:, h * HALF : (h + 1) * HALF]):
+                nc.scalar.activation(dst.rearrange("p (n c) -> p n c", c=CH), oldbank[:].rearrange("p c n -> p n c"), COPY)
 
         g01 = keep.tile([P, 2, S], BF16, name="g01")
         g23 = [keep.tile([P, 2, HALF], BF16, name="g23_%d" % h) for h in range(2)]
-        woven = [keep.tile([P, HALF, 4], BF16, name="woven%d" % h, align_bytes=64) for h in range(2)]
-        codes = [keep.tile([P, HALF], U32, name="codes%d" % h, align_bytes=64) for h in range(2)]
+        woven = [keep.tile([P, HALF, 4], BF16, name="woven%d" % h, tag="stage%d" % h, align_bytes=64) for h in range(2)]
+        codes = [keep.tile([P, HALF], U32, name="codes%d" % h, tag="late%d" % h, align_bytes=64) for h in range(2)]
         scales = [keep.tile([P, HALF], U8, name="scales%d" % h, align_bytes=64) for h in range(2)]
-        kept1 = keep.tile([P, S], F32, name="kept1")
         kept0 = keep.tile([P, S], F32, name="kept0")
         fresh0 = keep.tile([P, S], F32, name="fresh0")
 
         for j in range(2):
             nc.vector.tensor_copy(g01[:, j, :], planes[j][:].indirect(offs_sb[:]))
         for h in range(2):
-            nc.scalar.copy(woven[h][:, :, 0:2], g01[:, :, h * HALF : (h + 1) * HALF].rearrange("p j n -> p n j"))
-        for j in range(2):
-            for h in range(2):
-                nc.vector.tensor_copy(g23[h][:, j, :], planes[2 + j][:].indirect(offs_sb[:, h * LC : (h + 1) * LC]))
+            nc.scalar.copy(woven[h][:, :, 0:2].rearrange("p (c n) j -> p c n j", c=CH), g01[:, :, h * HALF : (h + 1) * HALF].rearrange("p j (n c) -> p c n j", c=CH))
         for h in range(2):
-            nc.scalar.copy(woven[h][:, :, 2:4], g23[h][:].rearrange("p j n -> p n j"))
+            nc.vector.tensor_copy(g23[h][:, 0, :], planes[2][:].indirect(offs_sb[:, h * LC : (h + 1) * LC]))
+        for h, lo, hi in ((0, 0, HALF), (1, 0, HALF)):
+            nc.vector.tensor_copy(g23[h][:, 1, lo:hi], planes[3][:].indirect(offs_sb[:, h * LC + lo // 16 : h * LC + hi // 16]))
+            nc.scalar.copy(
+                woven[h][:, :, 2:4].rearrange("p (c n) j -> p c n j", c=CH)[:, :, lo // CH : hi // CH, :],
+                g23[h][:, :, lo:hi].rearrange("p j (n c) -> p c n j", c=CH),
+            )
 
         for h in range(2):
             hs = slice(h * HALF, (h + 1) * HALF)
-            nc.vector.tensor_tensor(kept0[:, hs], mems[0][:].indirect(slot_sb[:, h * LC : (h + 1) * LC]), old_sb[:, hs], MULT)
+            nc.vector.tensor_tensor(kept0[:, hs], mems[0][:].indirect(slot_sb[:, h * LC : (h + 1) * LC]), old0[h][:], MULT)
             nc.vector.quantize_mx(out=codes[h][:].bitcast(FP8X4), scales=scales[h][:], in_=woven[h][:].rearrange("p n j -> p (n j)"))
-        nc.vector.tensor_tensor(kept1[:], mems[1][:].indirect(slot_sb[:]), old_sb[:], MULT)
+        kept1 = keep.tile([P, S], F32, name="kept1", tag="stage1", align_bytes=64)
+        nc.vector.tensor_tensor(kept1[:], mems[1][:].indirect(slot_sb[:]), old1[:], MULT)
 
         def fresh(b, h, dst):
             ybank = ypsum.tile([P, CH, P], F32, name="ybank", tag="ybank")
@@ -107,16 +110,15 @@ def tile_picked_ema_tanh_e_kernel(tc, xT, mem, w1_words, w1_scales, old, new, of
                     start=True,
                     stop=True,
                 )
-            y = keep.tile([P, CH, P], F32, name="y%d_%d" % (b, h))
+            y = keep.tile([P, CH, P], F32, name="y")
             nc.scalar.activation(y[:], ybank[:], TANH)
-            u = keep.tile([P, CH, P], F32, name="u%d_%d" % (b, h))
+            u = keep.tile([P, CH, P], F32, name="u")
             ubank = tpsum.tile([P, CH, P], F32, name="tbank", tag="tbank")
             for c in range(CH):
-                i = 8 + CH * h + c
-                nc.scalar.activation(u[:, c, :], y[:, c, :], COPY, scale=cols[:, i : i + 1])
+                nc.scalar.activation(u[:, c, :], y[:, c, :], COPY, scale=new_cols[:, h, c : c + 1])
             for c in range(CH):
                 nc.tensor.transpose(ubank[:, c, :], u[:, c, :], ident[:])
-            nc.scalar.copy(dst, ubank[:].rearrange("p c n -> p (c n)"))
+            nc.scalar.copy(dst.rearrange("p (n c) -> p n c", c=CH), ubank[:].rearrange("p c n -> p n c"))
 
         for h in range(2):
             hs = slice(h * HALF, (h + 1) * HALF)

@@ -29,8 +29,7 @@ def tile_picked_ema_tanh_e_kernel(tc, xT, mem, w1_words, w1_scales, old, new, of
     nc = tc.nc
     with ExitStack() as ctx:
         keep = ctx.enter_context(tc.tile_pool(name="keep", bufs=1))
-        ypsum = ctx.enter_context(tc.psum_pool(name="ypsum", bufs=4))
-        tpsum = ctx.enter_context(tc.psum_pool(name="tpsum", bufs=4))
+        psum = ctx.enter_context(tc.psum_pool(name="psum", bufs=1))
 
         offs_sb = keep.tile([P, S // 16], U16, name="offs_sb")
         slot_sb = keep.tile([P, S // 16], U16, name="slot_sb")
@@ -41,6 +40,9 @@ def tile_picked_ema_tanh_e_kernel(tc, xT, mem, w1_words, w1_scales, old, new, of
         old_cols = [keep.tile([P, CH], F32, name="old_cols%d" % h, tag="stage%d" % h, align_bytes=64) for h in range(2)]
         new_cols = keep.tile([P, 2, CH], F32, name="new_cols")
         ident = keep.tile([P, P], F32, name="ident")
+        banks = [psum.tile([P, CH, P], F32, name="bank%d" % i) for i in range(4)]
+        y = keep.tile([P, CH, P], F32, name="y")
+        u = keep.tile([P, CH, P], F32, name="u")
 
         nc.gpsimd.memset(w_scales[:].bitcast(I32), 0)
         make_identity(nc, ident[:])
@@ -51,54 +53,54 @@ def tile_picked_ema_tanh_e_kernel(tc, xT, mem, w1_words, w1_scales, old, new, of
         nc.sync.dma_start(offs_sb[:], offs)
         nc.sync.dma_start(planes[1][:], x_rows[:, 1, :])
         nc.sync.dma_start(planes[2][:], x_rows[:, 2, :])
-        nc.sync.dma_start(slot_sb[:], slot)
         nc.sync.dma_start(planes[3][:], x_rows[:, 3, :])
-        nc.sync.dma_start(mems[0][:], mem[0:P, :])
+        nc.sync.dma_start(slot_sb[:], slot)
+        nc.sync.dma_start(mems[1][:], mem[P : 2 * P, :])
         nc.sync.dma_start(w_words[:].bitcast(I32), w1_words[0].bitcast(I32))
         for q in range(4):
             nc.sync.dma_start(w_scales[32 * q : 32 * q + 4, :].bitcast(I32), w1_scales[0, 4 * q : 4 * q + 4, :].bitcast(I32))
-        nc.sync.dma_start(mems[1][:], mem[P : 2 * P, :])
+        nc.sync.dma_start(mems[0][:], mem[0:P, :])
         nc.sync.dma_start(new_cols[:], new[0:1, :].rearrange("o (h p c) -> (o p) h c", h=2, c=CH))
 
-        old1 = keep.tile([P, S], F32, name="old1")
-        old0 = [keep.tile([P, HALF], F32, name="old0_%d" % h, tag="late%d" % h, align_bytes=64) for h in range(2)]
+        old_all = keep.tile([P, S], F32, name="old_all")
+        old_first = keep.tile([P, HALF], F32, name="old_first", tag="late", align_bytes=64)
         for h in range(2):
-            oldbank = tpsum.tile([P, CH, P], F32, name="tbank", tag="tbank")
+            oldbank = banks[h]
             for c in range(CH):
                 nc.tensor.transpose(oldbank[:, c, :], old_cols[h][:, c : c + 1].to_broadcast([P, P]), ident[:])
-            for dst in (old0[h][:], old1[:, h * HALF : (h + 1) * HALF]):
+            for dst in [old_all[:, h * HALF : (h + 1) * HALF]] + ([old_first[:]] if h == 0 else []):
                 nc.scalar.activation(dst.rearrange("p (n c) -> p n c", c=CH), oldbank[:].rearrange("p c n -> p n c"), COPY)
 
         g01 = keep.tile([P, 2, S], BF16, name="g01")
-        g23 = [keep.tile([P, 2, HALF], BF16, name="g23_%d" % h) for h in range(2)]
+        g23 = keep.tile([P, 2, S], BF16, name="g23")
         woven = [keep.tile([P, HALF, 4], BF16, name="woven%d" % h, tag="stage%d" % h, align_bytes=64) for h in range(2)]
-        codes = [keep.tile([P, HALF], U32, name="codes%d" % h, tag="late%d" % h, align_bytes=64) for h in range(2)]
         scales = [keep.tile([P, HALF], U8, name="scales%d" % h, align_bytes=64) for h in range(2)]
-        kept0 = keep.tile([P, S], F32, name="kept0")
-        fresh0 = keep.tile([P, S], F32, name="fresh0")
+        kept = [keep.tile([P, S], F32, name="kept%d" % b) for b in range(2)]
 
-        for j in range(2):
-            nc.vector.tensor_copy(g01[:, j, :], planes[j][:].indirect(offs_sb[:]))
-        for h in range(2):
-            nc.scalar.copy(woven[h][:, :, 0:2].rearrange("p (c n) j -> p c n j", c=CH), g01[:, :, h * HALF : (h + 1) * HALF].rearrange("p j (n c) -> p c n j", c=CH))
-        for h in range(2):
-            nc.vector.tensor_copy(g23[h][:, 0, :], planes[2][:].indirect(offs_sb[:, h * LC : (h + 1) * LC]))
-        for h, lo, hi in ((0, 0, HALF), (1, 0, HALF)):
-            nc.vector.tensor_copy(g23[h][:, 1, lo:hi], planes[3][:].indirect(offs_sb[:, h * LC + lo // 16 : h * LC + hi // 16]))
-            nc.scalar.copy(
-                woven[h][:, :, 2:4].rearrange("p (c n) j -> p c n j", c=CH)[:, :, lo // CH : hi // CH, :],
-                g23[h][:, :, lo:hi].rearrange("p j (n c) -> p c n j", c=CH),
-            )
+        def gather_and_weave(pair, gathered, pieces):
+            nc.vector.tensor_copy(gathered[:, 0, :], planes[2 * pair][:].indirect(offs_sb[:]))
+            for lo, hi in pieces:
+                h = lo // HALF
+                nc.vector.tensor_copy(gathered[:, 1, lo:hi], planes[2 * pair + 1][:].indirect(offs_sb[:, lo // 16 : hi // 16]))
+                nc.scalar.copy(
+                    woven[h][:, :, 2 * pair : 2 * pair + 2].rearrange("p (c n) j -> p c n j", c=CH)[:, :, (lo - h * HALF) // CH : (hi - h * HALF) // CH, :],
+                    gathered[:, :, lo:hi].rearrange("p j (n c) -> p c n j", c=CH),
+                )
 
-        for h in range(2):
-            hs = slice(h * HALF, (h + 1) * HALF)
-            nc.vector.tensor_tensor(kept0[:, hs], mems[0][:].indirect(slot_sb[:, h * LC : (h + 1) * LC]), old0[h][:], MULT)
-            nc.vector.quantize_mx(out=codes[h][:].bitcast(FP8X4), scales=scales[h][:], in_=woven[h][:].rearrange("p n j -> p (n j)"))
-        kept1 = keep.tile([P, S], F32, name="kept1", tag="stage1", align_bytes=64)
-        nc.vector.tensor_tensor(kept1[:], mems[1][:].indirect(slot_sb[:]), old1[:], MULT)
+        gather_and_weave(0, g01, ((0, HALF), (HALF, S)))
+        gather_and_weave(1, g23, [(lo, lo + P) for lo in range(0, HALF, P)] + [(HALF, S)])
+
+        codes0 = keep.tile([P, HALF], U32, name="codes0", align_bytes=64)
+        nc.vector.quantize_mx(out=codes0[:].bitcast(FP8X4), scales=scales[0][:], in_=woven[0][:].rearrange("p n j -> p (n j)"))
+        nc.vector.tensor_tensor(kept[1][:, 0:HALF], mems[1][:].indirect(slot_sb[:, 0:LC]), old_first[:], MULT)
+        nc.vector.tensor_tensor(kept[1][:, HALF:S], mems[1][:].indirect(slot_sb[:, LC : 2 * LC]), old_all[:, HALF:S], MULT)
+        codes1 = keep.tile([P, HALF], U32, name="codes1", tag="late", align_bytes=64)
+        nc.vector.quantize_mx(out=codes1[:].bitcast(FP8X4), scales=scales[1][:], in_=woven[1][:].rearrange("p n j -> p (n j)"))
+        nc.vector.tensor_tensor(kept[0][:], mems[0][:].indirect(slot_sb[:]), old_all[:], MULT)
+        codes = [codes0, codes1]
 
         def fresh(b, h, dst):
-            ybank = ypsum.tile([P, CH, P], F32, name="ybank", tag="ybank")
+            ybank, ubank = banks[2 * b + h], banks[2 * b + 1 - h]
             for c in range(CH):
                 cs = slice(c * P, (c + 1) * P)
                 nc.tensor.matmul_mx(
@@ -110,10 +112,7 @@ def tile_picked_ema_tanh_e_kernel(tc, xT, mem, w1_words, w1_scales, old, new, of
                     start=True,
                     stop=True,
                 )
-            y = keep.tile([P, CH, P], F32, name="y")
             nc.scalar.activation(y[:], ybank[:], TANH)
-            u = keep.tile([P, CH, P], F32, name="u")
-            ubank = tpsum.tile([P, CH, P], F32, name="tbank", tag="tbank")
             for c in range(CH):
                 nc.scalar.activation(u[:, c, :], y[:, c, :], COPY, scale=new_cols[:, h, c : c + 1])
             for c in range(CH):
@@ -121,12 +120,9 @@ def tile_picked_ema_tanh_e_kernel(tc, xT, mem, w1_words, w1_scales, old, new, of
             nc.scalar.copy(dst.rearrange("p (n c) -> p n c", c=CH), ubank[:].rearrange("p c n -> p n c"))
 
         for h in range(2):
-            hs = slice(h * HALF, (h + 1) * HALF)
-            fresh1 = keep.tile([P, HALF], F32, name="fresh1_%d" % h)
-            fresh(1, h, fresh1[:])
-            nc.vector.tensor_tensor(mems[1][:].indirect(slot_sb[:, h * LC : (h + 1) * LC]), kept1[:, hs], fresh1[:], ADD)
-        nc.sync.dma_start(out[P : 2 * P, :], mems[1][:])
-        for h in range(2):
-            fresh(0, h, fresh0[:, h * HALF : (h + 1) * HALF])
-        nc.vector.tensor_tensor(mems[0][:].indirect(slot_sb[:]), kept0[:], fresh0[:], ADD)
-        nc.sync.dma_start(out[0:P, :], mems[0][:])
+            for b in (1, 0):
+                fresh_sb = keep.tile([P, HALF], F32, name="fresh%d_%d" % (b, h))
+                fresh(b, h, fresh_sb[:])
+                nc.vector.tensor_tensor(mems[b][:].indirect(slot_sb[:, h * LC : (h + 1) * LC]), kept[b][:, h * HALF : (h + 1) * HALF], fresh_sb[:], ADD)
+        for b in (1, 0):
+            nc.sync.dma_start(out[b * P : (b + 1) * P, :], mems[b][:])

@@ -21,8 +21,9 @@ ADD = mybir.AluOpType.add
 
 P = 128
 HALF = S // 2
-CH = HALF // P
-LC = HALF // 16
+QUARTER = S // 4
+CHUNKS = S // P
+LEAD = 64
 
 
 def tile_picked_ema_tanh_e_kernel(tc, xT, mem, w1_words, w1_scales, old, new, offs, slot, out):
@@ -37,21 +38,27 @@ def tile_picked_ema_tanh_e_kernel(tc, xT, mem, w1_words, w1_scales, old, new, of
         mems = [keep.tile([P, U], F32, name="mem%d" % b) for b in range(2)]
         w_words = keep.tile([P, 2 * N], U8, name="w_words", align_bytes=64)
         w_scales = keep.tile([P, N], U8, name="w_scales", align_bytes=64)
-        old_cols = [keep.tile([P, CH], F32, name="old_cols%d" % h, tag="stage%d" % h, align_bytes=64) for h in range(2)]
-        new_cols = keep.tile([P, 2, CH], F32, name="new_cols")
+        rows = keep.tile([P, P], F32, name="rows", tag="stage1", align_bytes=64)
+        old_cols = keep.tile([P, CHUNKS], F32, name="old_cols", tag="stage0", align_bytes=64)
+        new_cols = keep.tile([P, CHUNKS], F32, name="new_cols")
         ident = keep.tile([P, P], F32, name="ident")
-        banks = [psum.tile([P, CH, P], F32, name="bank%d" % i) for i in range(4)]
-        y = keep.tile([P, CH, P], F32, name="y")
-        u = keep.tile([P, CH, P], F32, name="u")
+        banks = [psum.tile([P, 4, P], F32, name="bank%d" % i) for i in range(4)]
 
-        nc.gpsimd.memset(w_scales[:].bitcast(I32), 0)
+        def offs_of(lo, hi):
+            return offs_sb[:, lo // 16 : hi // 16]
+
+        def slot_of(lo, hi):
+            return slot_sb[:, lo // 16 : hi // 16]
+
+        nc.gpsimd.memset(rows[:], 0.0)
         make_identity(nc, ident[:])
+        nc.gpsimd.memset(w_scales[:].bitcast(I32), 0)
         x_rows = xT.rearrange("(p j) t -> p j t", j=4)
-        for h in range(2):
-            nc.scalar.dma_start(old_cols[h][:], old[0:1, h * HALF : (h + 1) * HALF].rearrange("o (p c) -> (o p) c", c=CH))
+        nc.scalar.dma_start(old_cols[:], old[0:1, :].rearrange("o (p c) -> (o p) c", c=CHUNKS))
         nc.sync.dma_start(planes[0][:], x_rows[:, 0, :])
         nc.sync.dma_start(offs_sb[:], offs)
         nc.sync.dma_start(planes[1][:], x_rows[:, 1, :])
+        nc.sync.dma_start(rows[0:CHUNKS, :], new[0:1, :].rearrange("o (c n) -> (o c) n", n=P))
         nc.sync.dma_start(planes[2][:], x_rows[:, 2, :])
         nc.sync.dma_start(planes[3][:], x_rows[:, 3, :])
         nc.sync.dma_start(slot_sb[:], slot)
@@ -60,69 +67,95 @@ def tile_picked_ema_tanh_e_kernel(tc, xT, mem, w1_words, w1_scales, old, new, of
         for q in range(4):
             nc.sync.dma_start(w_scales[32 * q : 32 * q + 4, :].bitcast(I32), w1_scales[0, 4 * q : 4 * q + 4, :].bitcast(I32))
         nc.sync.dma_start(mems[0][:], mem[0:P, :])
-        nc.sync.dma_start(new_cols[:], new[0:1, :].rearrange("o (h p c) -> (o p) h c", h=2, c=CH))
 
         old_all = keep.tile([P, S], F32, name="old_all")
-        old_first = keep.tile([P, HALF], F32, name="old_first", tag="late", align_bytes=64)
+        old_first = [keep.tile([P, LEAD], F32, name="old_first%d" % b, tag="late%d" % b, align_bytes=64) for b in range(2)]
         for h in range(2):
-            oldbank = banks[h]
-            for c in range(CH):
-                nc.tensor.transpose(oldbank[:, c, :], old_cols[h][:, c : c + 1].to_broadcast([P, P]), ident[:])
-            for dst in [old_all[:, h * HALF : (h + 1) * HALF]] + ([old_first[:]] if h == 0 else []):
-                nc.scalar.activation(dst.rearrange("p (n c) -> p n c", c=CH), oldbank[:].rearrange("p c n -> p n c"), COPY)
+            oldbank = banks[1 + h]
+            for c in range(4):
+                nc.tensor.transpose(oldbank[:, c, :], old_cols[:, 4 * h + c : 4 * h + c + 1].to_broadcast([P, P]), ident[:])
+            nc.scalar.copy(old_all[:].rearrange("p (n c) -> p n c", c=CHUNKS)[:, :, 4 * h : 4 * h + 4], oldbank[:].rearrange("p c n -> p n c"))
+        for b in range(2):
+            nc.scalar.copy(old_first[b][:], old_all[:, 0:LEAD])
+        nc.tensor.transpose(banks[3][:, 0, :], rows[:], ident[:])
+        nc.scalar.copy(new_cols[:], banks[3][:, 0, 0:CHUNKS])
 
-        g01 = keep.tile([P, 2, S], BF16, name="g01")
-        g23 = keep.tile([P, 2, S], BF16, name="g23")
-        woven = [keep.tile([P, HALF, 4], BF16, name="woven%d" % h, tag="stage%d" % h, align_bytes=64) for h in range(2)]
-        scales = [keep.tile([P, HALF], U8, name="scales%d" % h, align_bytes=64) for h in range(2)]
+        gathered = keep.tile([P, 3 * S], BF16, name="gathered")
+        x3 = keep.tile([P, T], BF16, name="x3")
+        pieces = ((0, QUARTER), (QUARTER, HALF), (HALF, S))
+        halves = [keep.tile([P, HALF, 4], BF16, name="woven%d" % h, tag="stage%d" % h, align_bytes=64) for h in range(2)]
+        woven = [halves[0][:, 0:QUARTER, :], halves[0][:, QUARTER:HALF, :], halves[1][:]]
+        scales = [keep.tile([P, hi - lo], U8, name="scales%d" % i, align_bytes=64) for i, (lo, hi) in enumerate(pieces)]
         kept = [keep.tile([P, S], F32, name="kept%d" % b) for b in range(2)]
+        early = gathered[:].rearrange("p (j n) -> p n j", j=3)
+        parked = keep.tile([P, S], BF16, name="parked")[:]
 
-        def gather_and_weave(pair, gathered, pieces):
-            nc.vector.tensor_copy(gathered[:, 0, :], planes[2 * pair][:].indirect(offs_sb[:]))
-            for lo, hi in pieces:
-                h = lo // HALF
-                nc.vector.tensor_copy(gathered[:, 1, lo:hi], planes[2 * pair + 1][:].indirect(offs_sb[:, lo // 16 : hi // 16]))
-                nc.scalar.copy(
-                    woven[h][:, :, 2 * pair : 2 * pair + 2].rearrange("p (c n) j -> p c n j", c=CH)[:, :, (lo - h * HALF) // CH : (hi - h * HALF) // CH, :],
-                    gathered[:, :, lo:hi].rearrange("p j (n c) -> p c n j", c=CH),
-                )
+        def quantise(i, tag):
+            lo, hi = pieces[i]
+            codes.append(keep.tile([P, hi - lo], U32, name="codes%d" % i, tag=tag, align_bytes=64))
+            nc.vector.quantize_mx(out=codes[i][:].bitcast(FP8X4), scales=scales[i][:], in_=woven[i].rearrange("p n j -> p (n j)"))
 
-        gather_and_weave(0, g01, ((0, HALF), (HALF, S)))
-        gather_and_weave(1, g23, [(lo, lo + P) for lo in range(0, HALF, P)] + [(HALF, S)])
+        def keep_old(b, lo, hi, factor):
+            nc.vector.tensor_tensor(kept[b][:, lo:hi], mems[b][:].indirect(slot_of(lo, hi)), factor, MULT)
 
-        codes0 = keep.tile([P, HALF], U32, name="codes0", align_bytes=64)
-        nc.vector.quantize_mx(out=codes0[:].bitcast(FP8X4), scales=scales[0][:], in_=woven[0][:].rearrange("p n j -> p (n j)"))
-        nc.vector.tensor_tensor(kept[1][:, 0:HALF], mems[1][:].indirect(slot_sb[:, 0:LC]), old_first[:], MULT)
-        nc.vector.tensor_tensor(kept[1][:, HALF:S], mems[1][:].indirect(slot_sb[:, LC : 2 * LC]), old_all[:, HALF:S], MULT)
-        codes1 = keep.tile([P, HALF], U32, name="codes1", tag="late", align_bytes=64)
-        nc.vector.quantize_mx(out=codes1[:].bitcast(FP8X4), scales=scales[1][:], in_=woven[1][:].rearrange("p n j -> p (n j)"))
-        nc.vector.tensor_tensor(kept[0][:], mems[0][:].indirect(slot_sb[:]), old_all[:], MULT)
-        codes = [codes0, codes1]
+        codes = []
+        nc.vector.tensor_copy(gathered[:, 0:S], planes[0][:].indirect(offs_sb[:]))
+        nc.vector.tensor_copy(gathered[:, S : S + HALF], planes[1][:].indirect(offs_of(0, HALF)))
+        nc.scalar.copy(halves[0][:, :, 0:2], early[:, 0:HALF, 0:2])
+        nc.vector.tensor_copy(gathered[:, S + HALF : 2 * S], planes[1][:].indirect(offs_of(HALF, S)))
+        nc.vector.tensor_copy(gathered[:, 2 * S + HALF : 3 * S], planes[2][:].indirect(offs_of(HALF, S)))
+        nc.scalar.copy(woven[2][:, :, 0:3], early[:, HALF:S, :])
+        nc.vector.tensor_copy(parked[:, 0:HALF], planes[2][:].indirect(offs_of(0, HALF)))
+        for i in range(2):
+            lo, hi = pieces[i]
+            nc.vector.tensor_copy(parked[:, HALF + lo : HALF + hi], planes[3][:].indirect(offs_of(lo, hi)))
+            nc.scalar.copy(woven[i][:, :, 2:4], parked.rearrange("p (j n) -> p n j", j=2)[:, lo:hi, :])
+        nc.gpsimd.tensor_copy(x3[:, T // 2 : T], planes[3][:, T // 2 : T])
+        nc.vector.tensor_copy(x3[:, 0 : T // 2], planes[3][:, 0 : T // 2])
+        quantise(0, "early")
+        keep_old(1, 0, LEAD, old_first[1][:])
+        keep_old(1, LEAD, 6 * LEAD, old_all[:, LEAD : 6 * LEAD])
+        quantise(1, "late1")
+        keep_old(1, 6 * LEAD, S, old_all[:, 6 * LEAD : S])
+        keep_old(0, 0, LEAD, old_first[0][:])
+        keep_old(0, LEAD, S, old_all[:, LEAD:S])
+
+        def gather_last(lo, hi):
+            nc.scalar.activation(woven[2][:, lo - HALF : hi - HALF, 3], x3[:].indirect(offs_of(lo, hi)), COPY)
+
+        gather_last(HALF, HALF + QUARTER)
+        stages = [keep.tile([P, 4, P], F32, name="work%d" % i) for i in range(2)]
 
         def fresh(b, h, dst):
             ybank, ubank = banks[2 * b + h], banks[2 * b + 1 - h]
-            for c in range(CH):
-                cs = slice(c * P, (c + 1) * P)
+            y, u = stages if (b, h) == (1, 0) else stages[::-1]
+            for c in range(4):
+                i, place = (2, c) if h else divmod(c, 2)
+                cs = slice(place * P, (place + 1) * P)
                 nc.tensor.matmul_mx(
                     out=ybank[:, c, :],
-                    lhsT=codes[h][:, cs].bitcast(FP8X4),
-                    lhsT_scale=scales[h][:, cs],
+                    lhsT=codes[i][:, cs].bitcast(FP8X4),
+                    lhsT_scale=scales[i][:, cs],
                     rhs=w_words[:, 2 * P * b : 2 * P * (b + 1)].bitcast(FP4X4),
                     rhs_scale=w_scales[:, P * b : P * (b + 1)],
                     start=True,
                     stop=True,
                 )
             nc.scalar.activation(y[:], ybank[:], TANH)
-            for c in range(CH):
-                nc.scalar.activation(u[:, c, :], y[:, c, :], COPY, scale=new_cols[:, h, c : c + 1])
-            for c in range(CH):
+            for c in range(4):
+                nc.scalar.activation(u[:, c, :], y[:, c, :], COPY, scale=new_cols[:, 4 * h + c : 4 * h + c + 1])
+            for c in range(4):
                 nc.tensor.transpose(ubank[:, c, :], u[:, c, :], ident[:])
-            nc.scalar.copy(dst.rearrange("p (n c) -> p n c", c=CH), ubank[:].rearrange("p c n -> p n c"))
+            if (b, h) == (1, 0):
+                gather_last(HALF + QUARTER, S)
+                quantise(2, "late0")
+            nc.scalar.copy(dst, ubank[:].rearrange("p c n -> p (c n)"))
 
         for h in range(2):
+            lo, hi = h * HALF, (h + 1) * HALF
             for b in (1, 0):
                 fresh_sb = keep.tile([P, HALF], F32, name="fresh%d_%d" % (b, h))
                 fresh(b, h, fresh_sb[:])
-                nc.vector.tensor_tensor(mems[b][:].indirect(slot_sb[:, h * LC : (h + 1) * LC]), kept[b][:, h * HALF : (h + 1) * HALF], fresh_sb[:], ADD)
+                nc.vector.tensor_tensor(mems[b][:].indirect(slot_of(lo, hi)), kept[b][:, lo:hi], fresh_sb[:], ADD)
         for b in (1, 0):
             nc.sync.dma_start(out[b * P : (b + 1) * P, :], mems[b][:])

@@ -42,7 +42,7 @@ def tile_picked_ema_tanh_e_kernel(tc, xT, mem, w1_words, w1_scales, old, new, of
         old_cols = keep.tile([P, CHUNKS], F32, name="old_cols", tag="stage0", align_bytes=64)
         new_cols = keep.tile([P, CHUNKS], F32, name="new_cols")
         ident = keep.tile([P, P], F32, name="ident")
-        banks = [psum.tile([P, 4, P], F32, name="bank%d" % i) for i in range(4)]
+        banks = [psum.tile([P, 4, P], F32, name="bank%d" % i) for i in range(5)]
 
         def offs_of(lo, hi):
             return offs_sb[:, lo // 16 : hi // 16]
@@ -60,7 +60,8 @@ def tile_picked_ema_tanh_e_kernel(tc, xT, mem, w1_words, w1_scales, old, new, of
         nc.sync.dma_start(planes[1][:], x_rows[:, 1, :])
         nc.sync.dma_start(rows[0:CHUNKS, :], new[0:1, :].rearrange("o (c n) -> (o c) n", n=P))
         nc.sync.dma_start(planes[2][:], x_rows[:, 2, :])
-        nc.sync.dma_start(planes[3][:], x_rows[:, 3, :])
+        for lo in (0, T // 2):
+            nc.sync.dma_start(planes[3][:, lo : lo + T // 2], x_rows[:, 3, lo : lo + T // 2])
         nc.sync.dma_start(slot_sb[:], slot)
         nc.sync.dma_start(mems[1][:], mem[P : 2 * P, :])
         nc.sync.dma_start(w_words[:].bitcast(I32), w1_words[0].bitcast(I32))
@@ -90,10 +91,9 @@ def tile_picked_ema_tanh_e_kernel(tc, xT, mem, w1_words, w1_scales, old, new, of
         early = gathered[:].rearrange("p (j n) -> p n j", j=3)
         parked = keep.tile([P, S], BF16, name="parked")[:]
 
-        def quantise(i, tag):
-            lo, hi = pieces[i]
-            codes.append(keep.tile([P, hi - lo], U32, name="codes%d" % i, tag=tag, align_bytes=64))
-            nc.vector.quantize_mx(out=codes[i][:].bitcast(FP8X4), scales=scales[i][:], in_=woven[i].rearrange("p n j -> p (n j)"))
+        def quantise(i, words):
+            codes.append(words)
+            nc.vector.quantize_mx(out=words.bitcast(FP8X4), scales=scales[i][:], in_=woven[i].rearrange("p n j -> p (n j)"))
 
         def keep_old(b, lo, hi, factor):
             nc.vector.tensor_tensor(kept[b][:, lo:hi], mems[b][:].indirect(slot_of(lo, hi)), factor, MULT)
@@ -110,12 +110,13 @@ def tile_picked_ema_tanh_e_kernel(tc, xT, mem, w1_words, w1_scales, old, new, of
             lo, hi = pieces[i]
             nc.vector.tensor_copy(parked[:, HALF + lo : HALF + hi], planes[3][:].indirect(offs_of(lo, hi)))
             nc.scalar.copy(woven[i][:, :, 2:4], parked.rearrange("p (j n) -> p n j", j=2)[:, lo:hi, :])
-        nc.gpsimd.tensor_copy(x3[:, T // 2 : T], planes[3][:, T // 2 : T])
-        nc.vector.tensor_copy(x3[:, 0 : T // 2], planes[3][:, 0 : T // 2])
-        quantise(0, "early")
+        nc.gpsimd.tensor_copy(x3[:, 0 : T // 2], planes[3][:, 0 : T // 2])
+        nc.vector.tensor_copy(x3[:, T // 2 : T], planes[3][:, T // 2 : T])
         keep_old(1, 0, LEAD, old_first[1][:])
         keep_old(1, LEAD, 6 * LEAD, old_all[:, LEAD : 6 * LEAD])
-        quantise(1, "late1")
+        first_codes = keep.tile([P, HALF], U32, name="codes0", tag="late1", align_bytes=64)
+        for i in range(2):
+            quantise(i, first_codes[:, pieces[i][0] : pieces[i][1]])
         keep_old(1, 6 * LEAD, S, old_all[:, 6 * LEAD : S])
         keep_old(0, 0, LEAD, old_first[0][:])
         keep_old(0, LEAD, S, old_all[:, LEAD:S])
@@ -129,26 +130,29 @@ def tile_picked_ema_tanh_e_kernel(tc, xT, mem, w1_words, w1_scales, old, new, of
         def fresh(b, h, dst):
             ybank, ubank = banks[2 * b + h], banks[2 * b + 1 - h]
             y, u = stages if (b, h) == (1, 0) else stages[::-1]
-            for c in range(4):
-                i, place = (2, c) if h else divmod(c, 2)
-                cs = slice(place * P, (place + 1) * P)
-                nc.tensor.matmul_mx(
-                    out=ybank[:, c, :],
-                    lhsT=codes[i][:, cs].bitcast(FP8X4),
-                    lhsT_scale=scales[i][:, cs],
-                    rhs=w_words[:, 2 * P * b : 2 * P * (b + 1)].bitcast(FP4X4),
-                    rhs_scale=w_scales[:, P * b : P * (b + 1)],
-                    start=True,
-                    stop=True,
-                )
-            nc.scalar.activation(y[:], ybank[:], TANH)
-            for c in range(4):
-                nc.scalar.activation(u[:, c, :], y[:, c, :], COPY, scale=new_cols[:, 4 * h + c : 4 * h + c + 1])
+            groups = ((ybank, 0, 2), (banks[4], 2, 4)) if (b, h) == (1, 0) else ((ybank, 0, 4),)
+            for bank, first, last in groups:
+                for c in range(first, last):
+                    i, place = (2, c) if h else divmod(c, 2)
+                    cs = slice(place * P, (place + 1) * P)
+                    nc.tensor.matmul_mx(
+                        out=bank[:, c, :],
+                        lhsT=codes[i][:, cs].bitcast(FP8X4),
+                        lhsT_scale=scales[i][:, cs],
+                        rhs=w_words[:, 2 * P * b : 2 * P * (b + 1)].bitcast(FP4X4),
+                        rhs_scale=w_scales[:, P * b : P * (b + 1)],
+                        start=True,
+                        stop=True,
+                    )
+            for bank, first, last in groups:
+                nc.scalar.activation(y[:, first:last, :], bank[:, first:last, :], TANH)
+                for c in range(first, last):
+                    nc.scalar.activation(u[:, c, :], y[:, c, :], COPY, scale=new_cols[:, 4 * h + c : 4 * h + c + 1])
             for c in range(4):
                 nc.tensor.transpose(ubank[:, c, :], u[:, c, :], ident[:])
             if (b, h) == (1, 0):
                 gather_last(HALF + QUARTER, S)
-                quantise(2, "late0")
+                quantise(2, keep.tile([P, HALF], U32, name="codes1", tag="late0", align_bytes=64)[:])
             nc.scalar.copy(dst, ubank[:].rearrange("p c n -> p (c n)"))
 
         for h in range(2):

@@ -23,7 +23,6 @@ P = 128
 HALF = S // 2
 QUARTER = S // 4
 CHUNKS = S // P
-LEAD = 64
 
 
 def tile_picked_ema_tanh_e_kernel(tc, xT, mem, w1_words, w1_scales, old, new, offs, slot, out):
@@ -38,7 +37,7 @@ def tile_picked_ema_tanh_e_kernel(tc, xT, mem, w1_words, w1_scales, old, new, of
         mems = [keep.tile([P, U], F32, name="mem%d" % b) for b in range(2)]
         w_words = keep.tile([P, 2 * N], U8, name="w_words", align_bytes=64)
         w_scales = keep.tile([P, N], U8, name="w_scales", align_bytes=64)
-        rows = keep.tile([P, P], F32, name="rows", tag="stage1", align_bytes=64)
+        rows = keep.tile([P, P], F32, name="rows")
         old_cols = keep.tile([P, CHUNKS], F32, name="old_cols", tag="stage0", align_bytes=64)
         new_cols = keep.tile([P, CHUNKS], F32, name="new_cols")
         ident = keep.tile([P, P], F32, name="ident")
@@ -55,41 +54,37 @@ def tile_picked_ema_tanh_e_kernel(tc, xT, mem, w1_words, w1_scales, old, new, of
         nc.gpsimd.memset(w_scales[:].bitcast(I32), 0)
         x_rows = xT.rearrange("(p j) t -> p j t", j=4)
         nc.scalar.dma_start(old_cols[:], old[0:1, :].rearrange("o (p c) -> (o p) c", c=CHUNKS))
-        nc.sync.dma_start(planes[0][:], x_rows[:, 0, :])
-        nc.sync.dma_start(offs_sb[:], offs)
-        nc.sync.dma_start(planes[1][:], x_rows[:, 1, :])
-        nc.sync.dma_start(rows[0:CHUNKS, :], new[0:1, :].rearrange("o (c n) -> (o c) n", n=P))
         nc.sync.dma_start(planes[2][:], x_rows[:, 2, :])
+        nc.sync.dma_start(offs_sb[:], offs)
+        nc.sync.dma_start(planes[0][:], x_rows[:, 0, :])
+        nc.sync.dma_start(planes[1][:], x_rows[:, 1, :])
         for lo in (0, T // 2):
             nc.sync.dma_start(planes[3][:, lo : lo + T // 2], x_rows[:, 3, lo : lo + T // 2])
         nc.sync.dma_start(slot_sb[:], slot)
         nc.sync.dma_start(mems[1][:], mem[P : 2 * P, :])
+        nc.sync.dma_start(rows[0:CHUNKS, :], new[0:1, :].rearrange("o (c n) -> (o c) n", n=P))
         nc.sync.dma_start(w_words[:].bitcast(I32), w1_words[0].bitcast(I32))
         for q in range(4):
             nc.sync.dma_start(w_scales[32 * q : 32 * q + 4, :].bitcast(I32), w1_scales[0, 4 * q : 4 * q + 4, :].bitcast(I32))
         nc.sync.dma_start(mems[0][:], mem[0:P, :])
 
         old_all = keep.tile([P, S], F32, name="old_all")
-        old_first = [keep.tile([P, LEAD], F32, name="old_first%d" % b, tag="late%d" % b, align_bytes=64) for b in range(2)]
         for h in range(2):
             oldbank = banks[1 + h]
             for c in range(4):
                 nc.tensor.transpose(oldbank[:, c, :], old_cols[:, 4 * h + c : 4 * h + c + 1].to_broadcast([P, P]), ident[:])
             nc.scalar.copy(old_all[:].rearrange("p (n c) -> p n c", c=CHUNKS)[:, :, 4 * h : 4 * h + 4], oldbank[:].rearrange("p c n -> p n c"))
-        for b in range(2):
-            nc.scalar.copy(old_first[b][:], old_all[:, 0:LEAD])
-        nc.tensor.transpose(banks[3][:, 0, :], rows[:], ident[:])
-        nc.scalar.copy(new_cols[:], banks[3][:, 0, 0:CHUNKS])
 
-        gathered = keep.tile([P, 3 * S], BF16, name="gathered")
+        gathered = keep.tile([P, 2 * S], BF16, name="gathered")
+        x2 = keep.tile([P, T], BF16, name="x2")
         x3 = keep.tile([P, T], BF16, name="x3")
         pieces = ((0, QUARTER), (QUARTER, HALF), (HALF, S))
-        halves = [keep.tile([P, HALF, 4], BF16, name="woven%d" % h, tag="stage%d" % h, align_bytes=64) for h in range(2)]
-        woven = [halves[0][:, 0:QUARTER, :], halves[0][:, QUARTER:HALF, :], halves[1][:]]
+        first = keep.tile([P, HALF, 4], BF16, name="woven0", align_bytes=64)
+        second = keep.tile([P, HALF, 4], BF16, name="woven1", tag="stage0", align_bytes=64)
+        woven = [first[:, 0:QUARTER, :], first[:, QUARTER:HALF, :], second[:]]
         scales = [keep.tile([P, hi - lo], U8, name="scales%d" % i, align_bytes=64) for i, (lo, hi) in enumerate(pieces)]
         kept = [keep.tile([P, S], F32, name="kept%d" % b) for b in range(2)]
-        early = gathered[:].rearrange("p (j n) -> p n j", j=3)
-        parked = keep.tile([P, S], BF16, name="parked")[:]
+        early = gathered[:].rearrange("p (j n) -> p n j", j=2)
 
         def quantise(i, words):
             codes.append(words)
@@ -99,32 +94,34 @@ def tile_picked_ema_tanh_e_kernel(tc, xT, mem, w1_words, w1_scales, old, new, of
             nc.vector.tensor_tensor(kept[b][:, lo:hi], mems[b][:].indirect(slot_of(lo, hi)), factor, MULT)
 
         codes = []
+        nc.vector.tensor_copy(first[:, :, 2], planes[2][:].indirect(offs_of(0, HALF)))
+        nc.gpsimd.tensor_copy(x2[:, 0 : T // 2], planes[2][:, 0 : T // 2])
+        nc.vector.tensor_copy(x2[:, T // 2 : T], planes[2][:, T // 2 : T])
+        nc.scalar.activation(second[:, :, 2], x2[:].indirect(offs_of(HALF, S)), COPY)
         nc.vector.tensor_copy(gathered[:, 0:S], planes[0][:].indirect(offs_sb[:]))
         nc.vector.tensor_copy(gathered[:, S : S + HALF], planes[1][:].indirect(offs_of(0, HALF)))
-        nc.scalar.copy(halves[0][:, :, 0:2], early[:, 0:HALF, 0:2])
-        nc.vector.tensor_copy(gathered[:, S + HALF : 2 * S], planes[1][:].indirect(offs_of(HALF, S)))
-        nc.vector.tensor_copy(gathered[:, 2 * S + HALF : 3 * S], planes[2][:].indirect(offs_of(HALF, S)))
-        nc.scalar.copy(woven[2][:, :, 0:3], early[:, HALF:S, :])
-        nc.vector.tensor_copy(parked[:, 0:HALF], planes[2][:].indirect(offs_of(0, HALF)))
         for i in range(2):
             lo, hi = pieces[i]
-            nc.vector.tensor_copy(parked[:, HALF + lo : HALF + hi], planes[3][:].indirect(offs_of(lo, hi)))
-            nc.scalar.copy(woven[i][:, :, 2:4], parked.rearrange("p (j n) -> p n j", j=2)[:, lo:hi, :])
-        nc.gpsimd.tensor_copy(x3[:, 0 : T // 2], planes[3][:, 0 : T // 2])
-        nc.vector.tensor_copy(x3[:, T // 2 : T], planes[3][:, T // 2 : T])
-        keep_old(1, 0, LEAD, old_first[1][:])
-        keep_old(1, LEAD, 6 * LEAD, old_all[:, LEAD : 6 * LEAD])
-        first_codes = keep.tile([P, HALF], U32, name="codes0", tag="late1", align_bytes=64)
+            nc.scalar.copy(woven[i][:, :, 0:2], early[:, lo:hi, :])
+        nc.vector.tensor_copy(gathered[:, S + HALF : 2 * S], planes[1][:].indirect(offs_of(HALF, S)))
+        nc.scalar.copy(second[:, :, 0:2], early[:, HALF:S, :])
+        for i in range(2):
+            lo, hi = pieces[i]
+            nc.vector.tensor_copy(woven[i][:, :, 3], planes[3][:].indirect(offs_of(lo, hi)))
+        for lo in (0, T // 2):
+            nc.gpsimd.tensor_copy(x3[:, lo : lo + T // 2], planes[3][:, lo : lo + T // 2])
+        first_codes = keep.tile([P, HALF], U32, name="codes0", align_bytes=64)
         for i in range(2):
             quantise(i, first_codes[:, pieces[i][0] : pieces[i][1]])
-        keep_old(1, 6 * LEAD, S, old_all[:, 6 * LEAD : S])
-        keep_old(0, 0, LEAD, old_first[0][:])
-        keep_old(0, LEAD, S, old_all[:, LEAD:S])
+        keep_old(1, 0, S, old_all[:])
+        keep_old(0, 0, S, old_all[:])
 
         def gather_last(lo, hi):
-            nc.scalar.activation(woven[2][:, lo - HALF : hi - HALF, 3], x3[:].indirect(offs_of(lo, hi)), COPY)
+            nc.scalar.activation(second[:, lo - HALF : hi - HALF, 3], x3[:].indirect(offs_of(lo, hi)), COPY)
 
         gather_last(HALF, HALF + QUARTER)
+        nc.tensor.transpose(banks[3][:, 0, :], rows[:], ident[:])
+        nc.scalar.copy(new_cols[:], banks[3][:, 0, 0:CHUNKS])
         stages = [keep.tile([P, 4, P], F32, name="work%d" % i) for i in range(2)]
 
         def fresh(b, h, dst):
@@ -152,7 +149,7 @@ def tile_picked_ema_tanh_e_kernel(tc, xT, mem, w1_words, w1_scales, old, new, of
                 nc.tensor.transpose(ubank[:, c, :], u[:, c, :], ident[:])
             if (b, h) == (1, 0):
                 gather_last(HALF + QUARTER, S)
-                quantise(2, keep.tile([P, HALF], U32, name="codes1", tag="late0", align_bytes=64)[:])
+                quantise(2, keep.tile([P, HALF], U32, name="codes1", align_bytes=64)[:])
             nc.scalar.copy(dst, ubank[:].rearrange("p c n -> p (c n)"))
 
         for h in range(2):

@@ -37,11 +37,11 @@ def tile_picked_ema_tanh_e_kernel(tc, xT, mem, w1_words, w1_scales, old, new, of
         mems = [keep.tile([P, U], F32, name="mem%d" % b) for b in range(2)]
         w_words = keep.tile([P, 2 * N], U8, name="w_words", align_bytes=64)
         w_scales = keep.tile([P, N], U8, name="w_scales", align_bytes=64)
-        rows = keep.tile([P, P], F32, name="rows")
-        old_cols = keep.tile([P, CHUNKS], F32, name="old_cols", tag="stage0", align_bytes=64)
-        new_cols = keep.tile([P, CHUNKS], F32, name="new_cols")
+        old_cols = keep.tile([P, CHUNKS], F32, name="old_cols", tag="stage")
+        new_cols = keep.tile([P, 2, 4], F32, name="new_cols")
         ident = keep.tile([P, P], F32, name="ident")
-        banks = [psum.tile([P, 4, P], F32, name="bank%d" % i) for i in range(5)]
+        banks = [psum.tile([P, HALF], F32, name="bank%d" % i) for i in range(5)]
+        new_banks = [psum.tile([P, HALF], F32, name="new_bank%d" % h) for h in range(2)]
 
         def offs_of(lo, hi):
             return offs_sb[:, lo // 16 : hi // 16]
@@ -49,114 +49,133 @@ def tile_picked_ema_tanh_e_kernel(tc, xT, mem, w1_words, w1_scales, old, new, of
         def slot_of(lo, hi):
             return slot_sb[:, lo // 16 : hi // 16]
 
-        nc.gpsimd.memset(rows[:], 0.0)
+        nc.vector.memset(w_scales[:].bitcast(I32), 0)
         make_identity(nc, ident[:])
-        nc.gpsimd.memset(w_scales[:].bitcast(I32), 0)
         x_rows = xT.rearrange("(p j) t -> p j t", j=4)
-        nc.scalar.dma_start(old_cols[:], old[0:1, :].rearrange("o (p c) -> (o p) c", c=CHUNKS))
-        nc.sync.dma_start(planes[2][:], x_rows[:, 2, :])
-        nc.sync.dma_start(offs_sb[:], offs)
+        nc.sync.dma_start(old_cols[:], old[0:1, :].rearrange("o (p c) -> (o p) c", c=CHUNKS))
+        nc.scalar.dma_start(new_cols[:], new[0:1, :].rearrange("o (h p c) -> (o p) h c", h=2, c=4))
         nc.sync.dma_start(planes[0][:], x_rows[:, 0, :])
-        nc.sync.dma_start(planes[1][:], x_rows[:, 1, :])
-        for lo in (0, T // 2):
-            nc.sync.dma_start(planes[3][:, lo : lo + T // 2], x_rows[:, 3, lo : lo + T // 2])
+        nc.sync.dma_start(offs_sb[:], offs)
+        for j in range(1, 4):
+            nc.sync.dma_start(planes[j][:], x_rows[:, j, :])
         nc.sync.dma_start(slot_sb[:], slot)
-        nc.sync.dma_start(mems[1][:], mem[P : 2 * P, :])
-        nc.sync.dma_start(rows[0:CHUNKS, :], new[0:1, :].rearrange("o (c n) -> (o c) n", n=P))
+        nc.sync.dma_start(mems[0][:], mem[0:P, :])
         nc.sync.dma_start(w_words[:].bitcast(I32), w1_words[0].bitcast(I32))
         for q in range(4):
             nc.sync.dma_start(w_scales[32 * q : 32 * q + 4, :].bitcast(I32), w1_scales[0, 4 * q : 4 * q + 4, :].bitcast(I32))
-        nc.sync.dma_start(mems[0][:], mem[0:P, :])
+        nc.sync.dma_start(mems[1][:], mem[P : 2 * P, :])
 
         old_all = keep.tile([P, S], F32, name="old_all")
         for h in range(2):
-            oldbank = banks[1 + h]
+            bank = banks[h][:].rearrange("p (c n) -> p c n", c=4)
             for c in range(4):
-                nc.tensor.transpose(oldbank[:, c, :], old_cols[:, 4 * h + c : 4 * h + c + 1].to_broadcast([P, P]), ident[:])
-            nc.scalar.copy(old_all[:].rearrange("p (n c) -> p n c", c=CHUNKS)[:, :, 4 * h : 4 * h + 4], oldbank[:].rearrange("p c n -> p n c"))
-
-        gathered = keep.tile([P, 2 * S], BF16, name="gathered")
-        x2 = keep.tile([P, T], BF16, name="x2")
-        x3 = keep.tile([P, T], BF16, name="x3")
-        pieces = ((0, QUARTER), (QUARTER, HALF), (HALF, S))
-        first = keep.tile([P, HALF, 4], BF16, name="woven0", align_bytes=64)
-        second = keep.tile([P, HALF, 4], BF16, name="woven1", tag="stage0", align_bytes=64)
-        woven = [first[:, 0:QUARTER, :], first[:, QUARTER:HALF, :], second[:]]
-        scales = [keep.tile([P, hi - lo], U8, name="scales%d" % i, align_bytes=64) for i, (lo, hi) in enumerate(pieces)]
-        kept = [keep.tile([P, S], F32, name="kept%d" % b) for b in range(2)]
-        early = gathered[:].rearrange("p (j n) -> p n j", j=2)
-
-        def quantise(i, words):
-            codes.append(words)
-            nc.vector.quantize_mx(out=words.bitcast(FP8X4), scales=scales[i][:], in_=woven[i].rearrange("p n j -> p (n j)"))
-
-        def keep_old(b, lo, hi, factor):
-            nc.vector.tensor_tensor(kept[b][:, lo:hi], mems[b][:].indirect(slot_of(lo, hi)), factor, MULT)
-
-        codes = []
-        nc.vector.tensor_copy(first[:, :, 2], planes[2][:].indirect(offs_of(0, HALF)))
-        nc.gpsimd.tensor_copy(x2[:, 0 : T // 2], planes[2][:, 0 : T // 2])
-        nc.vector.tensor_copy(x2[:, T // 2 : T], planes[2][:, T // 2 : T])
-        nc.scalar.activation(second[:, :, 2], x2[:].indirect(offs_of(HALF, S)), COPY)
-        nc.vector.tensor_copy(gathered[:, 0:S], planes[0][:].indirect(offs_sb[:]))
-        nc.vector.tensor_copy(gathered[:, S : S + HALF], planes[1][:].indirect(offs_of(0, HALF)))
-        for i in range(2):
-            lo, hi = pieces[i]
-            nc.scalar.copy(woven[i][:, :, 0:2], early[:, lo:hi, :])
-        nc.vector.tensor_copy(gathered[:, S + HALF : 2 * S], planes[1][:].indirect(offs_of(HALF, S)))
-        nc.scalar.copy(second[:, :, 0:2], early[:, HALF:S, :])
-        for i in range(2):
-            lo, hi = pieces[i]
-            nc.vector.tensor_copy(woven[i][:, :, 3], planes[3][:].indirect(offs_of(lo, hi)))
-        for lo in (0, T // 2):
-            nc.gpsimd.tensor_copy(x3[:, lo : lo + T // 2], planes[3][:, lo : lo + T // 2])
-        first_codes = keep.tile([P, HALF], U32, name="codes0", align_bytes=64)
-        for i in range(2):
-            quantise(i, first_codes[:, pieces[i][0] : pieces[i][1]])
-        keep_old(1, 0, S, old_all[:])
-        keep_old(0, 0, S, old_all[:])
-
-        def gather_last(lo, hi):
-            nc.scalar.activation(second[:, lo - HALF : hi - HALF, 3], x3[:].indirect(offs_of(lo, hi)), COPY)
-
-        gather_last(HALF, HALF + QUARTER)
-        nc.tensor.transpose(banks[3][:, 0, :], rows[:], ident[:])
-        nc.scalar.copy(new_cols[:], banks[3][:, 0, 0:CHUNKS])
-        stages = [keep.tile([P, 4, P], F32, name="work%d" % i) for i in range(2)]
-
-        def fresh(b, h, dst):
-            ybank, ubank = banks[2 * b + h], banks[2 * b + 1 - h]
-            y, u = stages if (b, h) == (1, 0) else stages[::-1]
-            groups = ((ybank, 0, 2), (banks[4], 2, 4)) if (b, h) == (1, 0) else ((ybank, 0, 4),)
-            for bank, first, last in groups:
-                for c in range(first, last):
-                    i, place = (2, c) if h else divmod(c, 2)
-                    cs = slice(place * P, (place + 1) * P)
-                    nc.tensor.matmul_mx(
-                        out=bank[:, c, :],
-                        lhsT=codes[i][:, cs].bitcast(FP8X4),
-                        lhsT_scale=scales[i][:, cs],
-                        rhs=w_words[:, 2 * P * b : 2 * P * (b + 1)].bitcast(FP4X4),
-                        rhs_scale=w_scales[:, P * b : P * (b + 1)],
-                        start=True,
-                        stop=True,
-                    )
-            for bank, first, last in groups:
-                nc.scalar.activation(y[:, first:last, :], bank[:, first:last, :], TANH)
-                for c in range(first, last):
-                    nc.scalar.activation(u[:, c, :], y[:, c, :], COPY, scale=new_cols[:, 4 * h + c : 4 * h + c + 1])
-            for c in range(4):
-                nc.tensor.transpose(ubank[:, c, :], u[:, c, :], ident[:])
-            if (b, h) == (1, 0):
-                gather_last(HALF + QUARTER, S)
-                quantise(2, keep.tile([P, HALF], U32, name="codes1", align_bytes=64)[:])
-            nc.scalar.copy(dst, ubank[:].rearrange("p c n -> p (c n)"))
-
+                nc.tensor.transpose(bank[:, c, :], old_cols[:, 4 * h + c : 4 * h + c + 1].to_broadcast([P, P]), ident[:])
+            nc.scalar.copy(old_all[:].rearrange("p (n c) -> p n c", c=CHUNKS)[:, :, 4 * h : 4 * h + 4], bank.rearrange("p c n -> p n c"))
         for h in range(2):
-            lo, hi = h * HALF, (h + 1) * HALF
-            for b in (1, 0):
-                fresh_sb = keep.tile([P, HALF], F32, name="fresh%d_%d" % (b, h))
-                fresh(b, h, fresh_sb[:])
-                nc.vector.tensor_tensor(mems[b][:].indirect(slot_of(lo, hi)), kept[b][:, lo:hi], fresh_sb[:], ADD)
-        for b in (1, 0):
-            nc.sync.dma_start(out[b * P : (b + 1) * P, :], mems[b][:])
+            for c in range(4):
+                nc.tensor.transpose(new_banks[h][:, c:HALF:4], new_cols[:, h, c : c + 1].to_broadcast([P, P]), ident[:])
+
+        pieces = ((0, 256), (256, 512), (512, 1024))
+        woven = [keep.tile([P, hi - lo, 4], BF16, name="woven%d" % lo, align_bytes=64) for lo, hi in pieces]
+        front = keep.tile([P, 2, S], BF16, name="front", tag="stage")
+        backs = [keep.tile([P, 2, hi - lo], BF16, name="back%d" % lo) for lo, hi in pieces[1:]]
+        codes = [keep.tile([P, hi - lo], U32, name="codes%d" % lo, tag="codes%d" % lo, align_bytes=64) for lo, hi in pieces]
+        scales = [keep.tile([P, hi - lo], U8, name="scales%d" % lo, align_bytes=64) for lo, hi in pieces]
+
+        def weave(i):
+            nc.vector.tensor_copy(woven[i][:, :, 2:4], backs[i - 1][:].rearrange("p j n -> p n j"))
+
+        for j in range(2):
+            nc.vector.tensor_copy(front[:, j, 0:HALF], planes[j][:].indirect(offs_of(0, HALF)))
+            nc.scalar.activation(front[:, j, HALF:S], planes[j][:].indirect(offs_of(HALF, S)), COPY)
+        for i, (lo, hi) in reversed(list(enumerate(pieces))):
+            nc.vector.tensor_copy(woven[i][:, :, 0:2], front[:, :, lo:hi].rearrange("p j n -> p n j"))
+        for j in range(2, 4):
+            nc.vector.tensor_copy(woven[0][:, :, j], planes[j][:].indirect(offs_of(*pieces[0])))
+            for i in range(1, len(pieces)):
+                nc.scalar.activation(backs[i - 1][:, j - 2, :], planes[j][:].indirect(offs_of(*pieces[i])), COPY)
+
+        def quantise(i):
+            nc.vector.quantize_mx(out=codes[i][:].bitcast(FP8X4), scales=scales[i][:], in_=woven[i][:].rearrange("p n j -> p (n j)"))
+
+        acts = [keep.tile([P, S], F32, name="act%d" % b) for b in range(2)]
+        fresh = [keep.tile([P, S], F32, name="fresh%d" % b) for b in range(2)]
+        kept = [keep.tile([P, S], F32, name="kept%d" % b) for b in range(2)]
+        summed = [keep.tile([P, S], F32, name="summed0")]
+
+        def result(b, lo, hi):
+            h = lo // HALF
+            bank = banks[4] if (b, lo) == (0, 0) else banks[2 * b + h]
+            return bank[:, lo - h * HALF : hi - h * HALF]
+
+        def project(b, i):
+            nc.tensor.matmul_mx(
+                out=result(b, *pieces[i]),
+                lhsT=w_words[:, 2 * P * b : 2 * P * (b + 1)].bitcast(FP4X4),
+                lhsT_scale=w_scales[:, P * b : P * (b + 1)],
+                rhs=codes[i][:].bitcast(FP8X4),
+                rhs_scale=scales[i][:],
+                start=True,
+                stop=True,
+            )
+
+        def squash(b, lo, hi):
+            nc.scalar.activation(acts[b][:, lo:hi], result(b, lo, hi), TANH)
+
+        def weigh(b, lo, hi):
+            h = lo // HALF
+            nc.vector.tensor_tensor(fresh[b][:, lo:hi], acts[b][:, lo:hi], new_banks[h][:, lo - h * HALF : hi - h * HALF], MULT)
+
+        def keep_old(b, lo, hi):
+            nc.vector.tensor_tensor(kept[b][:, lo:hi], mems[b][:].indirect(slot_of(lo, hi)), old_all[:, lo:hi], MULT)
+
+        def scalar_put(b, lo, hi):
+            nc.scalar.activation(mems[b][:].indirect(slot_of(lo, hi)), summed[b][:, lo:hi], COPY)
+
+        def vector_put(b, lo, hi):
+            nc.vector.tensor_tensor(mems[b][:].indirect(slot_of(lo, hi)), kept[b][:, lo:hi], fresh[b][:, lo:hi], ADD)
+
+        def look_up(h, dst):
+            nc.scalar.activation(dst[:], mems[0][:].indirect(slot_of(h * HALF, (h + 1) * HALF)), COPY)
+
+        def decay(h, src):
+            nc.vector.tensor_tensor(kept[0][:, h * HALF : (h + 1) * HALF], src[:], old_all[:, h * HALF : (h + 1) * HALF], MULT)
+
+        def add_up(lo, hi):
+            nc.vector.tensor_tensor(summed[0][:, lo:hi], kept[0][:, lo:hi], fresh[0][:, lo:hi], ADD)
+
+        weave(1)
+        quantise(0)
+        quantise(1)
+        weave(2)
+        quantise(2)
+        for i in range(3):
+            for b in range(2):
+                project(b, i)
+        looked = [keep.tile([P, HALF], F32, name="looked0"), keep.tile([P, HALF], F32, name="looked1", tag="codes256", align_bytes=64)]
+        look_up(0, looked[0])
+        squash(0, 0, QUARTER)
+        squash(0, QUARTER, HALF)
+        look_up(1, looked[1])
+        decay(0, looked[0])
+        weigh(0, 0, QUARTER)
+        weigh(0, QUARTER, HALF)
+        add_up(0, QUARTER)
+        add_up(QUARTER, HALF)
+        scalar_put(0, 0, QUARTER)
+        squash(0, HALF, S)
+        decay(1, looked[1])
+        keep_old(1, 0, HALF)
+        weigh(0, HALF, S)
+        keep_old(1, HALF, S)
+        add_up(HALF, S)
+        scalar_put(0, QUARTER, HALF)
+        squash(1, 0, HALF)
+        squash(1, HALF, S)
+        scalar_put(0, HALF, HALF + QUARTER)
+        scalar_put(0, HALF + QUARTER, S)
+        nc.sync.dma_start(out[0:P, :], mems[0][:])
+        weigh(1, 0, HALF)
+        weigh(1, HALF, S)
+        vector_put(1, 0, S)
+        nc.sync.dma_start(out[P : 2 * P, :], mems[1][:])

@@ -37,11 +37,10 @@ def tile_picked_ema_tanh_e_kernel(tc, xT, mem, w1_words, w1_scales, old, new, of
         mems = [keep.tile([P, U], F32, name="mem%d" % b) for b in range(2)]
         w_words = keep.tile([P, 2 * N], U8, name="w_words", align_bytes=64)
         w_scales = keep.tile([P, N], U8, name="w_scales", align_bytes=64)
-        old_cols = keep.tile([P, CHUNKS], F32, name="old_cols", tag="stage")
-        new_cols = keep.tile([P, 2, 4], F32, name="new_cols")
+        cols = [keep.tile([P, 2, 4], F32, name="old_cols", tag="stage"), keep.tile([P, 2, 4], F32, name="new_cols")]
         ident = keep.tile([P, P], F32, name="ident")
-        banks = [psum.tile([P, HALF], F32, name="bank%d" % i) for i in range(5)]
-        new_banks = [psum.tile([P, HALF], F32, name="new_bank%d" % h) for h in range(2)]
+        banks = [psum.tile([P, HALF], F32, name="bank%d" % i) for i in range(4)]
+        spread = [[psum.tile([P, HALF], F32, name="spread%d_%d" % (i, h)) for h in range(2)] for i in range(2)]
 
         def offs_of(lo, hi):
             return offs_sb[:, lo // 16 : hi // 16]
@@ -49,11 +48,11 @@ def tile_picked_ema_tanh_e_kernel(tc, xT, mem, w1_words, w1_scales, old, new, of
         def slot_of(lo, hi):
             return slot_sb[:, lo // 16 : hi // 16]
 
-        nc.vector.memset(w_scales[:].bitcast(I32), 0)
+        nc.gpsimd.memset(w_scales[:].bitcast(I32), 0)
         make_identity(nc, ident[:])
         x_rows = xT.rearrange("(p j) t -> p j t", j=4)
-        nc.sync.dma_start(old_cols[:], old[0:1, :].rearrange("o (p c) -> (o p) c", c=CHUNKS))
-        nc.scalar.dma_start(new_cols[:], new[0:1, :].rearrange("o (h p c) -> (o p) h c", h=2, c=4))
+        for queue, tile, factor in ((nc.sync, cols[0], old), (nc.scalar, cols[1], new)):
+            queue.dma_start(tile[:], factor[0:1, :].rearrange("o (h p c) -> (o p) h c", h=2, c=4))
         nc.sync.dma_start(planes[0][:], x_rows[:, 0, :])
         nc.sync.dma_start(offs_sb[:], offs)
         for j in range(1, 4):
@@ -66,18 +65,16 @@ def tile_picked_ema_tanh_e_kernel(tc, xT, mem, w1_words, w1_scales, old, new, of
         nc.sync.dma_start(mems[1][:], mem[P : 2 * P, :])
 
         old_all = keep.tile([P, S], F32, name="old_all")
+        for i in range(2):
+            for h in range(2):
+                for c in range(4):
+                    nc.tensor.transpose(spread[i][h][:, c:HALF:4], cols[i][:, h, c : c + 1].to_broadcast([P, P]), ident[:])
         for h in range(2):
-            bank = banks[h][:].rearrange("p (c n) -> p c n", c=4)
-            for c in range(4):
-                nc.tensor.transpose(bank[:, c, :], old_cols[:, 4 * h + c : 4 * h + c + 1].to_broadcast([P, P]), ident[:])
-            nc.scalar.copy(old_all[:].rearrange("p (n c) -> p n c", c=CHUNKS)[:, :, 4 * h : 4 * h + 4], bank.rearrange("p c n -> p n c"))
-        for h in range(2):
-            for c in range(4):
-                nc.tensor.transpose(new_banks[h][:, c:HALF:4], new_cols[:, h, c : c + 1].to_broadcast([P, P]), ident[:])
+            nc.scalar.copy(old_all[:, h * HALF : (h + 1) * HALF], spread[0][h][:])
 
-        pieces = ((0, 256), (256, 512), (512, 1024))
-        woven = [keep.tile([P, hi - lo, 4], BF16, name="woven%d" % lo, align_bytes=64) for lo, hi in pieces]
-        front = keep.tile([P, 2, S], BF16, name="front", tag="stage")
+        pieces = ((0, HALF), (HALF, S))
+        woven = [keep.tile([P, hi - lo, 4], BF16, name="woven%d" % lo, tag="woven%d" % lo, align_bytes=64) for lo, hi in pieces]
+        fronts = [keep.tile([P, 2, HALF], BF16, name="front0"), keep.tile([P, 2, HALF], BF16, name="front1", tag="stage")]
         backs = [keep.tile([P, 2, hi - lo], BF16, name="back%d" % lo) for lo, hi in pieces[1:]]
         codes = [keep.tile([P, hi - lo], U32, name="codes%d" % lo, tag="codes%d" % lo, align_bytes=64) for lo, hi in pieces]
         scales = [keep.tile([P, hi - lo], U8, name="scales%d" % lo, align_bytes=64) for lo, hi in pieces]
@@ -86,10 +83,10 @@ def tile_picked_ema_tanh_e_kernel(tc, xT, mem, w1_words, w1_scales, old, new, of
             nc.vector.tensor_copy(woven[i][:, :, 2:4], backs[i - 1][:].rearrange("p j n -> p n j"))
 
         for j in range(2):
-            nc.vector.tensor_copy(front[:, j, 0:HALF], planes[j][:].indirect(offs_of(0, HALF)))
-            nc.scalar.activation(front[:, j, HALF:S], planes[j][:].indirect(offs_of(HALF, S)), COPY)
+            nc.vector.tensor_copy(fronts[0][:, j, :], planes[j][:].indirect(offs_of(0, HALF)))
+            nc.scalar.activation(fronts[1][:, j, :], planes[j][:].indirect(offs_of(HALF, S)), COPY)
         for i, (lo, hi) in reversed(list(enumerate(pieces))):
-            nc.vector.tensor_copy(woven[i][:, :, 0:2], front[:, :, lo:hi].rearrange("p j n -> p n j"))
+            nc.vector.tensor_copy(woven[i][:, :, 0:2], fronts[i][:].rearrange("p j n -> p n j"))
         for j in range(2, 4):
             nc.vector.tensor_copy(woven[0][:, :, j], planes[j][:].indirect(offs_of(*pieces[0])))
             for i in range(1, len(pieces)):
@@ -98,84 +95,71 @@ def tile_picked_ema_tanh_e_kernel(tc, xT, mem, w1_words, w1_scales, old, new, of
         def quantise(i):
             nc.vector.quantize_mx(out=codes[i][:].bitcast(FP8X4), scales=scales[i][:], in_=woven[i][:].rearrange("p n j -> p (n j)"))
 
-        acts = [keep.tile([P, S], F32, name="act%d" % b) for b in range(2)]
+        acts = {(b, h): keep.tile([P, HALF], F32, name="act%d_%d" % (b, h), tag="act%d_%d" % (b, h)) for b in range(2) for h in range(2)}
+        looked = [keep.tile([P, HALF], F32, name="looked%d" % h) for h in range(2)]
         fresh = [keep.tile([P, S], F32, name="fresh%d" % b) for b in range(2)]
-        kept = [keep.tile([P, S], F32, name="kept%d" % b) for b in range(2)]
-        summed = [keep.tile([P, S], F32, name="summed0")]
+        kept = keep.tile([P, S], F32, name="kept")
+        summed = keep.tile([P, S], F32, name="summed")
 
-        def result(b, lo, hi):
-            h = lo // HALF
-            bank = banks[4] if (b, lo) == (0, 0) else banks[2 * b + h]
-            return bank[:, lo - h * HALF : hi - h * HALF]
+        def half(tile, h):
+            return tile[:, h * HALF : (h + 1) * HALF]
 
-        def project(b, i):
+        def project(b, h):
             nc.tensor.matmul_mx(
-                out=result(b, *pieces[i]),
+                out=banks[2 * b + h][:],
                 lhsT=w_words[:, 2 * P * b : 2 * P * (b + 1)].bitcast(FP4X4),
                 lhsT_scale=w_scales[:, P * b : P * (b + 1)],
-                rhs=codes[i][:].bitcast(FP8X4),
-                rhs_scale=scales[i][:],
+                rhs=codes[h][:].bitcast(FP8X4),
+                rhs_scale=scales[h][:],
                 start=True,
                 stop=True,
             )
 
-        def squash(b, lo, hi):
-            nc.scalar.activation(acts[b][:, lo:hi], result(b, lo, hi), TANH)
+        def squash(b, h):
+            nc.scalar.activation(acts[(b, h)][:], banks[2 * b + h][:], TANH)
 
-        def weigh(b, lo, hi):
-            h = lo // HALF
-            nc.vector.tensor_tensor(fresh[b][:, lo:hi], acts[b][:, lo:hi], new_banks[h][:, lo - h * HALF : hi - h * HALF], MULT)
+        def look_up(h):
+            nc.scalar.activation(looked[h][:], mems[0][:].indirect(slot_of(h * HALF, (h + 1) * HALF)), COPY)
 
-        def keep_old(b, lo, hi):
-            nc.vector.tensor_tensor(kept[b][:, lo:hi], mems[b][:].indirect(slot_of(lo, hi)), old_all[:, lo:hi], MULT)
+        def decay(h):
+            nc.vector.tensor_tensor(half(kept, h), looked[h][:], spread[0][h][:], MULT)
 
-        def scalar_put(b, lo, hi):
-            nc.scalar.activation(mems[b][:].indirect(slot_of(lo, hi)), summed[b][:, lo:hi], COPY)
+        def weigh(b, h):
+            nc.vector.tensor_tensor(half(fresh[b], h), acts[(b, h)][:], spread[1][h][:], MULT)
 
-        def vector_put(b, lo, hi):
-            nc.vector.tensor_tensor(mems[b][:].indirect(slot_of(lo, hi)), kept[b][:, lo:hi], fresh[b][:, lo:hi], ADD)
+        def add_up(h):
+            nc.gpsimd.tensor_tensor(half(summed, h), half(kept, h), half(fresh[0], h), ADD)
 
-        def look_up(h, dst):
-            nc.scalar.activation(dst[:], mems[0][:].indirect(slot_of(h * HALF, (h + 1) * HALF)), COPY)
-
-        def decay(h, src):
-            nc.vector.tensor_tensor(kept[0][:, h * HALF : (h + 1) * HALF], src[:], old_all[:, h * HALF : (h + 1) * HALF], MULT)
-
-        def add_up(lo, hi):
-            nc.vector.tensor_tensor(summed[0][:, lo:hi], kept[0][:, lo:hi], fresh[0][:, lo:hi], ADD)
+        def keep_old(dst, lo, hi):
+            nc.vector.tensor_tensor(dst[:], mems[1][:].indirect(slot_of(lo, hi)), old_all[:, lo:hi], MULT)
 
         weave(1)
         quantise(0)
         quantise(1)
-        weave(2)
-        quantise(2)
-        for i in range(3):
+        for h in range(2):
             for b in range(2):
-                project(b, i)
-        looked = [keep.tile([P, HALF], F32, name="looked0"), keep.tile([P, HALF], F32, name="looked1", tag="codes256", align_bytes=64)]
-        look_up(0, looked[0])
-        squash(0, 0, QUARTER)
-        squash(0, QUARTER, HALF)
-        look_up(1, looked[1])
-        decay(0, looked[0])
-        weigh(0, 0, QUARTER)
-        weigh(0, QUARTER, HALF)
-        add_up(0, QUARTER)
-        add_up(QUARTER, HALF)
-        scalar_put(0, 0, QUARTER)
-        squash(0, HALF, S)
-        decay(1, looked[1])
-        keep_old(1, 0, HALF)
-        weigh(0, HALF, S)
-        keep_old(1, HALF, S)
-        add_up(HALF, S)
-        scalar_put(0, QUARTER, HALF)
-        squash(1, 0, HALF)
-        squash(1, HALF, S)
-        scalar_put(0, HALF, HALF + QUARTER)
-        scalar_put(0, HALF + QUARTER, S)
+                project(b, h)
+        look_up(0)
+        squash(0, 0)
+        look_up(1)
+        squash(0, 1)
+        squash(1, 0)
+        squash(1, 1)
+        decay(0)
+        weigh(0, 0)
+        add_up(0)
+        early = keep.tile([P, QUARTER], F32, name="early")
+        keep_old(early, 0, QUARTER)
+        decay(1)
+        weigh(0, 1)
+        add_up(1)
+        weigh(1, 0)
+        weigh(1, 1)
+        late = keep.tile([P, S - QUARTER], F32, name="late", tag="act1_0")
+        keep_old(late, QUARTER, S)
+        for lo, hi in ((0, 384), (384, 768), (768, S)):
+            nc.scalar.activation(mems[0][:].indirect(slot_of(lo, hi)), summed[:, lo:hi], COPY)
         nc.sync.dma_start(out[0:P, :], mems[0][:])
-        weigh(1, 0, HALF)
-        weigh(1, HALF, S)
-        vector_put(1, 0, S)
+        for part, lo, hi in ((early, 0, QUARTER), (late, QUARTER, S)):
+            nc.vector.tensor_tensor(mems[1][:].indirect(slot_of(lo, hi)), part[:], fresh[1][:, lo:hi], ADD)
         nc.sync.dma_start(out[P : 2 * P, :], mems[1][:])

@@ -23,6 +23,7 @@ P = 128
 HALF = S // 2
 QUARTER = S // 4
 CHUNKS = S // P
+FREE = P - 2 * CHUNKS
 
 
 def tile_picked_ema_tanh_e_kernel(tc, xT, mem, w1_words, w1_scales, old, new, offs, slot, out):
@@ -37,7 +38,8 @@ def tile_picked_ema_tanh_e_kernel(tc, xT, mem, w1_words, w1_scales, old, new, of
         mems = [keep.tile([P, U], F32, name="mem%d" % b) for b in range(2)]
         w_words = keep.tile([P, 2 * N], U8, name="w_words", align_bytes=64)
         w_scales = keep.tile([P, N], U8, name="w_scales", align_bytes=64)
-        cols = [keep.tile([P, 2, 4], F32, name="old_cols", tag="stage"), keep.tile([P, 2, 4], F32, name="new_cols")]
+        rows = keep.tile([P, P], F32, name="rows", tag="stage")
+        cols = keep.tile([P, 2 * CHUNKS], F32, name="cols")
         ident = keep.tile([P, P], F32, name="ident")
         banks = [psum.tile([P, HALF], F32, name="bank%d" % i) for i in range(4)]
         spread = [[psum.tile([P, HALF], F32, name="spread%d_%d" % (i, h)) for h in range(2)] for i in range(2)]
@@ -48,11 +50,12 @@ def tile_picked_ema_tanh_e_kernel(tc, xT, mem, w1_words, w1_scales, old, new, of
         def slot_of(lo, hi):
             return slot_sb[:, lo // 16 : hi // 16]
 
+        nc.gpsimd.memset(rows[0:FREE, :], 0.0)
         nc.gpsimd.memset(w_scales[:].bitcast(I32), 0)
         make_identity(nc, ident[:])
         x_rows = xT.rearrange("(p j) t -> p j t", j=4)
-        for queue, tile, factor in ((nc.sync, cols[0], old), (nc.scalar, cols[1], new)):
-            queue.dma_start(tile[:], factor[0:1, :].rearrange("o (h p c) -> (o p) h c", h=2, c=4))
+        for i, factor in enumerate((old, new)):
+            nc.scalar.dma_start(rows[FREE + i * CHUNKS : FREE + (i + 1) * CHUNKS, :], factor[0:1, :].rearrange("o (c n) -> (o c) n", n=P))
         nc.sync.dma_start(planes[0][:], x_rows[:, 0, :])
         nc.sync.dma_start(offs_sb[:], offs)
         for j in range(1, 4):
@@ -65,10 +68,11 @@ def tile_picked_ema_tanh_e_kernel(tc, xT, mem, w1_words, w1_scales, old, new, of
         nc.sync.dma_start(mems[1][:], mem[P : 2 * P, :])
 
         old_all = keep.tile([P, S], F32, name="old_all")
-        for i in range(2):
-            for h in range(2):
-                for c in range(4):
-                    nc.tensor.transpose(spread[i][h][:, c:HALF:4], cols[i][:, h, c : c + 1].to_broadcast([P, P]), ident[:])
+        nc.tensor.transpose(banks[0][:, 0:P], rows[:], ident[:])
+        nc.scalar.copy(cols[:], banks[0][:, FREE:P])
+        for c in range(2 * CHUNKS):
+            i, h, place = c // CHUNKS, c % CHUNKS // 4, c % 4
+            nc.tensor.transpose(spread[i][h][:, place * P : (place + 1) * P], cols[:, c : c + 1].to_broadcast([P, P]), ident[:])
         for h in range(2):
             nc.scalar.copy(old_all[:, h * HALF : (h + 1) * HALF], spread[0][h][:])
 
@@ -85,7 +89,7 @@ def tile_picked_ema_tanh_e_kernel(tc, xT, mem, w1_words, w1_scales, old, new, of
         for j in range(2):
             nc.vector.tensor_copy(fronts[0][:, j, :], planes[j][:].indirect(offs_of(0, HALF)))
             nc.scalar.activation(fronts[1][:, j, :], planes[j][:].indirect(offs_of(HALF, S)), COPY)
-        for i, (lo, hi) in reversed(list(enumerate(pieces))):
+        for i in range(2):
             nc.vector.tensor_copy(woven[i][:, :, 0:2], fronts[i][:].rearrange("p j n -> p n j"))
         for j in range(2, 4):
             nc.vector.tensor_copy(woven[0][:, :, j], planes[j][:].indirect(offs_of(*pieces[0])))

@@ -100,7 +100,6 @@ def tile_picked_ema_tanh_e_kernel(tc, xT, mem, w1_words, w1_scales, old, new, of
             nc.vector.quantize_mx(out=codes[i][:].bitcast(FP8X4), scales=scales[i][:], in_=woven[i][:].rearrange("p n j -> p (n j)"))
 
         acts = {(b, h): keep.tile([P, HALF], F32, name="act%d_%d" % (b, h), tag="act%d_%d" % (b, h)) for b in range(2) for h in range(2)}
-        looked = [keep.tile([P, HALF], F32, name="looked%d" % h) for h in range(2)]
         fresh = [keep.tile([P, S], F32, name="fresh%d" % b) for b in range(2)]
         kept = keep.tile([P, S], F32, name="kept")
         summed = keep.tile([P, S], F32, name="summed")
@@ -143,6 +142,7 @@ def tile_picked_ema_tanh_e_kernel(tc, xT, mem, w1_words, w1_scales, old, new, of
         for h in range(2):
             for b in range(2):
                 project(b, h)
+        looked = [keep.tile([P, HALF], F32, name="looked0"), keep.tile([P, HALF], F32, name="looked1", tag="codes0", align_bytes=64)]
         look_up(0)
         squash(0, 0)
         look_up(1)
@@ -152,18 +152,15 @@ def tile_picked_ema_tanh_e_kernel(tc, xT, mem, w1_words, w1_scales, old, new, of
         decay(0)
         weigh(0, 0)
         add_up(0)
-        early = keep.tile([P, QUARTER], F32, name="early")
-        keep_old(early, 0, QUARTER)
         decay(1)
         weigh(0, 1)
         add_up(1)
         weigh(1, 0)
         weigh(1, 1)
-        late = keep.tile([P, S - QUARTER], F32, name="late", tag="act1_0")
-        keep_old(late, QUARTER, S)
+        late = keep.tile([P, S], F32, name="late", tag="act1_0")
+        keep_old(late, 0, S)
         for lo, hi in ((0, 384), (384, 768), (768, S)):
             nc.scalar.activation(mems[0][:].indirect(slot_of(lo, hi)), summed[:, lo:hi], COPY)
         nc.sync.dma_start(out[0:P, :], mems[0][:])
-        for part, lo, hi in ((early, 0, QUARTER), (late, QUARTER, S)):
-            nc.vector.tensor_tensor(mems[1][:].indirect(slot_of(lo, hi)), part[:], fresh[1][:, lo:hi], ADD)
+        nc.vector.tensor_tensor(mems[1][:].indirect(slot_sb[:]), late[:], fresh[1][:], ADD)
         nc.sync.dma_start(out[P : 2 * P, :], mems[1][:])

@@ -78,7 +78,7 @@ def tile_picked_ema_tanh_e_kernel(tc, xT, mem, w1_words, w1_scales, old, new, of
 
         pieces = ((0, HALF), (HALF, S))
         woven = [keep.tile([P, hi - lo, 4], BF16, name="woven%d" % lo, tag="woven%d" % lo, align_bytes=64) for lo, hi in pieces]
-        fronts = [keep.tile([P, 2, HALF], BF16, name="front0"), keep.tile([P, 2, HALF], BF16, name="front1", tag="stage")]
+        front = keep.tile([P, 2, HALF], BF16, name="front", tag="stage")
         backs = [keep.tile([P, 2, hi - lo], BF16, name="back%d" % lo) for lo, hi in pieces[1:]]
         codes = [keep.tile([P, hi - lo], U32, name="codes%d" % lo, tag="codes%d" % lo, align_bytes=64) for lo, hi in pieces]
         scales = [keep.tile([P, hi - lo], U8, name="scales%d" % lo, align_bytes=64) for lo, hi in pieces]
@@ -87,10 +87,9 @@ def tile_picked_ema_tanh_e_kernel(tc, xT, mem, w1_words, w1_scales, old, new, of
             nc.vector.tensor_copy(woven[i][:, :, 2:4], backs[i - 1][:].rearrange("p j n -> p n j"))
 
         for j in range(2):
-            nc.vector.tensor_copy(fronts[0][:, j, :], planes[j][:].indirect(offs_of(0, HALF)))
-            nc.scalar.activation(fronts[1][:, j, :], planes[j][:].indirect(offs_of(HALF, S)), COPY)
-        for i in range(2):
-            nc.vector.tensor_copy(woven[i][:, :, 0:2], fronts[i][:].rearrange("p j n -> p n j"))
+            nc.vector.tensor_copy(woven[0][:, :, j], planes[j][:].indirect(offs_of(0, HALF)))
+            nc.scalar.activation(front[:, j, :], planes[j][:].indirect(offs_of(HALF, S)), COPY)
+        nc.vector.tensor_copy(woven[1][:, :, 0:2], front[:].rearrange("p j n -> p n j"))
         for j in range(2, 4):
             nc.vector.tensor_copy(woven[0][:, :, j], planes[j][:].indirect(offs_of(*pieces[0])))
             for i in range(1, len(pieces)):
@@ -103,6 +102,8 @@ def tile_picked_ema_tanh_e_kernel(tc, xT, mem, w1_words, w1_scales, old, new, of
         fresh = [keep.tile([P, S], F32, name="fresh%d" % b) for b in range(2)]
         kept = keep.tile([P, S], F32, name="kept")
         summed = keep.tile([P, S], F32, name="summed")
+
+        spans = ((0, HALF), (HALF, S - P))
 
         def half(tile, h):
             return tile[:, h * HALF : (h + 1) * HALF]
@@ -122,10 +123,11 @@ def tile_picked_ema_tanh_e_kernel(tc, xT, mem, w1_words, w1_scales, old, new, of
             nc.scalar.activation(acts[(b, h)][:], banks[2 * b + h][:], TANH)
 
         def look_up(h):
-            nc.scalar.activation(looked[h][:], mems[0][:].indirect(slot_of(h * HALF, (h + 1) * HALF)), COPY)
+            nc.scalar.activation(looked[h][:], mems[0][:].indirect(slot_of(*spans[h])), COPY)
 
         def decay(h):
-            nc.vector.tensor_tensor(half(kept, h), looked[h][:], spread[0][h][:], MULT)
+            lo, hi = spans[h]
+            nc.vector.tensor_tensor(kept[:, lo:hi], looked[h][:], spread[0][h][:, 0 : hi - lo], MULT)
 
         def weigh(b, h):
             nc.vector.tensor_tensor(half(fresh[b], h), acts[(b, h)][:], spread[1][h][:], MULT)
@@ -133,8 +135,8 @@ def tile_picked_ema_tanh_e_kernel(tc, xT, mem, w1_words, w1_scales, old, new, of
         def add_up(h):
             nc.gpsimd.tensor_tensor(half(summed, h), half(kept, h), half(fresh[0], h), ADD)
 
-        def keep_old(dst, lo, hi):
-            nc.vector.tensor_tensor(dst[:], mems[1][:].indirect(slot_of(lo, hi)), old_all[:, lo:hi], MULT)
+        def keep_old(dst, b, lo, hi):
+            nc.vector.tensor_tensor(dst, mems[b][:].indirect(slot_of(lo, hi)), old_all[:, lo:hi], MULT)
 
         weave(1)
         quantise(0)
@@ -142,7 +144,8 @@ def tile_picked_ema_tanh_e_kernel(tc, xT, mem, w1_words, w1_scales, old, new, of
         for h in range(2):
             for b in range(2):
                 project(b, h)
-        looked = [keep.tile([P, HALF], F32, name="looked0"), keep.tile([P, HALF], F32, name="looked1", tag="codes0", align_bytes=64)]
+        looked = [keep.tile([P, HALF], F32, name="looked0"), keep.tile([P, HALF - P], F32, name="looked1", tag="codes0", align_bytes=64)]
+        keep_old(kept[:, S - P : S], 0, S - P, S)
         look_up(0)
         squash(0, 0)
         look_up(1)
@@ -158,7 +161,7 @@ def tile_picked_ema_tanh_e_kernel(tc, xT, mem, w1_words, w1_scales, old, new, of
         weigh(1, 0)
         weigh(1, 1)
         late = keep.tile([P, S], F32, name="late", tag="act1_0")
-        keep_old(late, 0, S)
+        keep_old(late[:], 1, 0, S)
         for lo, hi in ((0, 384), (384, 768), (768, S)):
             nc.scalar.activation(mems[0][:].indirect(slot_of(lo, hi)), summed[:, lo:hi], COPY)
         nc.sync.dma_start(out[0:P, :], mems[0][:])

@@ -23,7 +23,9 @@ P = 128
 HALF = S // 2
 QUARTER = S // 4
 CHUNKS = S // P
-FREE = P - 2 * CHUNKS
+CLEARED = P - 2 * CHUNKS
+SCALAR_LOOKS_UP = S - P
+SCATTER_PIECE = 384
 
 
 def tile_picked_ema_tanh_e_kernel(tc, xT, mem, w1_words, w1_scales, old, new, offs, slot, out):
@@ -50,12 +52,14 @@ def tile_picked_ema_tanh_e_kernel(tc, xT, mem, w1_words, w1_scales, old, new, of
         def slot_of(lo, hi):
             return slot_sb[:, lo // 16 : hi // 16]
 
-        nc.gpsimd.memset(rows[0:FREE, :], 0.0)
+        nc.gpsimd.memset(rows[0:CLEARED, :], 0.0)
         nc.gpsimd.memset(w_scales[:].bitcast(I32), 0)
         make_identity(nc, ident[:])
         x_rows = xT.rearrange("(p j) t -> p j t", j=4)
         for i, factor in enumerate((old, new)):
-            nc.scalar.dma_start(rows[FREE + i * CHUNKS : FREE + (i + 1) * CHUNKS, :], factor[0:1, :].rearrange("o (c n) -> (o c) n", n=P))
+            first = CLEARED + i * CHUNKS
+            nc.scalar.dma_start(rows[first : first + CHUNKS, :], factor[0:1, :].rearrange("o (c n) -> (o c) n", n=P))
+
         nc.sync.dma_start(planes[0][:], x_rows[:, 0, :])
         nc.sync.dma_start(offs_sb[:], offs)
         for j in range(1, 4):
@@ -69,101 +73,91 @@ def tile_picked_ema_tanh_e_kernel(tc, xT, mem, w1_words, w1_scales, old, new, of
 
         old_all = keep.tile([P, S], F32, name="old_all")
         nc.tensor.transpose(banks[0][:, 0:P], rows[:], ident[:])
-        nc.scalar.copy(cols[:], banks[0][:, FREE:P])
+        nc.scalar.copy(cols[:], banks[0][:, CLEARED:P])
         for c in range(2 * CHUNKS):
             i, h, place = c // CHUNKS, c % CHUNKS // 4, c % 4
             nc.tensor.transpose(spread[i][h][:, place * P : (place + 1) * P], cols[:, c : c + 1].to_broadcast([P, P]), ident[:])
         for h in range(2):
             nc.scalar.copy(old_all[:, h * HALF : (h + 1) * HALF], spread[0][h][:])
 
-        pieces = ((0, HALF), (HALF, S))
-        woven = [keep.tile([P, hi - lo, 4], BF16, name="woven%d" % lo, tag="woven%d" % lo, align_bytes=64) for lo, hi in pieces]
+        woven = [keep.tile([P, HALF, 4], BF16, name="woven%d" % lo, tag="woven%d" % lo, align_bytes=64) for lo in (0, HALF)]
         front = keep.tile([P, 2, HALF], BF16, name="front", tag="stage")
-        backs = [keep.tile([P, 2, hi - lo], BF16, name="back%d" % lo) for lo, hi in pieces[1:]]
-        codes = [keep.tile([P, hi - lo], U32, name="codes%d" % lo, tag="codes%d" % lo, align_bytes=64) for lo, hi in pieces]
-        scales = [keep.tile([P, hi - lo], U8, name="scales%d" % lo, align_bytes=64) for lo, hi in pieces]
-
-        def weave(i):
-            nc.vector.tensor_copy(woven[i][:, :, 2:4], backs[i - 1][:].rearrange("p j n -> p n j"))
+        backs = [keep.tile([P, 2, QUARTER], BF16, name="back%d" % q) for q in range(2)]
+        codes = [keep.tile([P, HALF], U32, name="codes%d" % lo, tag="codes%d" % lo, align_bytes=64) for lo in (0, HALF)]
+        scales = [keep.tile([P, HALF], U8, name="scales%d" % lo, align_bytes=64) for lo in (0, HALF)]
 
         for j in range(2):
             nc.vector.tensor_copy(woven[0][:, :, j], planes[j][:].indirect(offs_of(0, HALF)))
             nc.scalar.activation(front[:, j, :], planes[j][:].indirect(offs_of(HALF, S)), COPY)
         nc.vector.tensor_copy(woven[1][:, :, 0:2], front[:].rearrange("p j n -> p n j"))
         for j in range(2, 4):
-            nc.vector.tensor_copy(woven[0][:, :, j], planes[j][:].indirect(offs_of(*pieces[0])))
-            for i in range(1, len(pieces)):
-                nc.scalar.activation(backs[i - 1][:, j - 2, :], planes[j][:].indirect(offs_of(*pieces[i])), COPY)
-
-        def quantise(i):
-            nc.vector.quantize_mx(out=codes[i][:].bitcast(FP8X4), scales=scales[i][:], in_=woven[i][:].rearrange("p n j -> p (n j)"))
+            nc.vector.tensor_copy(woven[0][:, :, j], planes[j][:].indirect(offs_of(0, HALF)))
+            for q in (1, 0):
+                lo = HALF + q * QUARTER
+                nc.scalar.activation(backs[q][:, j - 2, :], planes[j][:].indirect(offs_of(lo, lo + QUARTER)), COPY)
+        nc.scalar.copy(woven[1][:, QUARTER:HALF, 2:4], backs[1][:].rearrange("p j n -> p n j"))
+        nc.vector.tensor_copy(woven[1][:, 0:QUARTER, 2:4], backs[0][:].rearrange("p j n -> p n j"))
 
         acts = {(b, h): keep.tile([P, HALF], F32, name="act%d_%d" % (b, h), tag="act%d_%d" % (b, h)) for b in range(2) for h in range(2)}
         fresh = [keep.tile([P, S], F32, name="fresh%d" % b) for b in range(2)]
         kept = keep.tile([P, S], F32, name="kept")
         summed = keep.tile([P, S], F32, name="summed")
-
-        spans = ((0, HALF), (HALF, S - P))
+        scalar_spans = ((0, HALF), (HALF, SCALAR_LOOKS_UP))
 
         def half(tile, h):
             return tile[:, h * HALF : (h + 1) * HALF]
-
-        def project(b, h):
-            nc.tensor.matmul_mx(
-                out=banks[2 * b + h][:],
-                lhsT=w_words[:, 2 * P * b : 2 * P * (b + 1)].bitcast(FP4X4),
-                lhsT_scale=w_scales[:, P * b : P * (b + 1)],
-                rhs=codes[h][:].bitcast(FP8X4),
-                rhs_scale=scales[h][:],
-                start=True,
-                stop=True,
-            )
 
         def squash(b, h):
             nc.scalar.activation(acts[(b, h)][:], banks[2 * b + h][:], TANH)
 
         def look_up(h):
-            nc.scalar.activation(looked[h][:], mems[0][:].indirect(slot_of(*spans[h])), COPY)
-
-        def decay(h):
-            lo, hi = spans[h]
-            nc.vector.tensor_tensor(kept[:, lo:hi], looked[h][:], spread[0][h][:, 0 : hi - lo], MULT)
+            nc.scalar.activation(looked[h][:], mems[0][:].indirect(slot_of(*scalar_spans[h])), COPY)
 
         def weigh(b, h):
             nc.vector.tensor_tensor(half(fresh[b], h), acts[(b, h)][:], spread[1][h][:], MULT)
 
-        def add_up(h):
-            nc.gpsimd.tensor_tensor(half(summed, h), half(kept, h), half(fresh[0], h), ADD)
-
-        def keep_old(dst, b, lo, hi):
+        def gather_times_old(dst, b, lo, hi):
             nc.vector.tensor_tensor(dst, mems[b][:].indirect(slot_of(lo, hi)), old_all[:, lo:hi], MULT)
 
-        weave(1)
-        quantise(0)
-        quantise(1)
+        for h in range(2):
+            nc.vector.quantize_mx(out=codes[h][:].bitcast(FP8X4), scales=scales[h][:], in_=woven[h][:].rearrange("p n j -> p (n j)"))
         for h in range(2):
             for b in range(2):
-                project(b, h)
-        looked = [keep.tile([P, HALF], F32, name="looked0"), keep.tile([P, HALF - P], F32, name="looked1", tag="codes0", align_bytes=64)]
-        keep_old(kept[:, S - P : S], 0, S - P, S)
+                nc.tensor.matmul_mx(
+                    out=banks[2 * b + h][:],
+                    lhsT=w_words[:, 2 * P * b : 2 * P * (b + 1)].bitcast(FP4X4),
+                    lhsT_scale=w_scales[:, P * b : P * (b + 1)],
+                    rhs=codes[h][:].bitcast(FP8X4),
+                    rhs_scale=scales[h][:],
+                    start=True,
+                    stop=True,
+                )
+
+        looked = [
+            keep.tile([P, HALF], F32, name="looked0"),
+            keep.tile([P, SCALAR_LOOKS_UP - HALF], F32, name="looked1", tag="codes0", align_bytes=64),
+        ]
+        gather_times_old(kept[:, SCALAR_LOOKS_UP:S], 0, SCALAR_LOOKS_UP, S)
         look_up(0)
         squash(0, 0)
         look_up(1)
         squash(0, 1)
-        squash(1, 0)
-        squash(1, 1)
-        decay(0)
-        weigh(0, 0)
-        add_up(0)
-        decay(1)
-        weigh(0, 1)
-        add_up(1)
-        weigh(1, 0)
-        weigh(1, 1)
-        late = keep.tile([P, S], F32, name="late", tag="act1_0")
-        keep_old(late[:], 1, 0, S)
-        for lo, hi in ((0, 384), (384, 768), (768, S)):
+        for h in range(2):
+            squash(1, h)
+        for h in range(2):
+            lo, hi = scalar_spans[h]
+            nc.vector.tensor_tensor(kept[:, lo:hi], looked[h][:], spread[0][h][:, 0 : hi - lo], MULT)
+            weigh(0, h)
+            nc.gpsimd.tensor_tensor(half(summed, h), half(kept, h), half(fresh[0], h), ADD)
+
+        for h in range(2):
+            weigh(1, h)
+        kept_second = keep.tile([P, S], F32, name="late", tag="act1_0")
+        gather_times_old(kept_second[:], 1, 0, S)
+
+        for lo in range(0, S, SCATTER_PIECE):
+            hi = min(lo + SCATTER_PIECE, S)
             nc.scalar.activation(mems[0][:].indirect(slot_of(lo, hi)), summed[:, lo:hi], COPY)
         nc.sync.dma_start(out[0:P, :], mems[0][:])
-        nc.vector.tensor_tensor(mems[1][:].indirect(slot_sb[:]), late[:], fresh[1][:], ADD)
+        nc.vector.tensor_tensor(mems[1][:].indirect(slot_sb[:]), kept_second[:], fresh[1][:], ADD)
         nc.sync.dma_start(out[P : 2 * P, :], mems[1][:])

@@ -24,7 +24,7 @@ HALF = S // 2
 QUARTER = S // 4
 CHUNKS = S // P
 CLEARED = P - 2 * CHUNKS
-SCALAR_LOOKS_UP = S - P
+FUSED = (HALF, HALF + QUARTER)
 SCATTER_PIECE = 384
 
 
@@ -65,64 +65,46 @@ def tile_picked_ema_tanh_e_kernel(tc, xT, mem, w1_words, w1_scales, old, new, of
         for j in range(1, 4):
             nc.sync.dma_start(planes[j][:], x_rows[:, j, :])
         nc.sync.dma_start(slot_sb[:], slot)
-        nc.sync.dma_start(mems[0][:], mem[0:P, :])
-        nc.sync.dma_start(w_words[:].bitcast(I32), w1_words[0].bitcast(I32))
         for q in range(4):
             nc.sync.dma_start(w_scales[32 * q : 32 * q + 4, :].bitcast(I32), w1_scales[0, 4 * q : 4 * q + 4, :].bitcast(I32))
+        nc.sync.dma_start(mems[0][:], mem[0:P, :])
+        nc.sync.dma_start(w_words[:].bitcast(I32), w1_words[0].bitcast(I32))
         nc.sync.dma_start(mems[1][:], mem[P : 2 * P, :])
 
-        old_all = keep.tile([P, S], F32, name="old_all")
+        old_first = keep.tile([P, FUSED[1]], F32, name="old_first")
         nc.tensor.transpose(banks[0][:, 0:P], rows[:], ident[:])
         nc.scalar.copy(cols[:], banks[0][:, CLEARED:P])
         for c in range(2 * CHUNKS):
             i, h, place = c // CHUNKS, c % CHUNKS // 4, c % 4
             nc.tensor.transpose(spread[i][h][:, place * P : (place + 1) * P], cols[:, c : c + 1].to_broadcast([P, P]), ident[:])
-        for h in range(2):
-            nc.scalar.copy(old_all[:, h * HALF : (h + 1) * HALF], spread[0][h][:])
+        nc.vector.tensor_copy(old_first[:, 0:HALF], spread[0][0][:])
+        nc.vector.tensor_copy(old_first[:, HALF : FUSED[1]], spread[0][1][:, 0 : FUSED[1] - HALF])
 
-        woven = [keep.tile([P, HALF, 4], BF16, name="woven%d" % lo, tag="woven%d" % lo, align_bytes=64) for lo in (0, HALF)]
+        woven = [keep.tile([P, HALF, 4], BF16, name="woven%d" % h, tag="woven%d" % h, align_bytes=64) for h in range(2)]
         front = keep.tile([P, 2, HALF], BF16, name="front", tag="stage")
         backs = [keep.tile([P, 2, QUARTER], BF16, name="back%d" % q) for q in range(2)]
-        codes = [keep.tile([P, HALF], U32, name="codes%d" % lo, tag="codes%d" % lo, align_bytes=64) for lo in (0, HALF)]
-        scales = [keep.tile([P, HALF], U8, name="scales%d" % lo, align_bytes=64) for lo in (0, HALF)]
+        codes = [keep.tile([P, HALF], U32, name="codes%d" % h, tag="codes%d" % h, align_bytes=64) for h in range(2)]
+        scales = [keep.tile([P, HALF], U8, name="scales%d" % h, align_bytes=64) for h in range(2)]
+
+        def pairs(rows_of_two_planes):
+            return rows_of_two_planes.rearrange("p j n -> p n j")
 
         for j in range(2):
             nc.vector.tensor_copy(woven[0][:, :, j], planes[j][:].indirect(offs_of(0, HALF)))
             nc.scalar.activation(front[:, j, :], planes[j][:].indirect(offs_of(HALF, S)), COPY)
-        nc.vector.tensor_copy(woven[1][:, :, 0:2], front[:].rearrange("p j n -> p n j"))
+        nc.gpsimd.tensor_copy(woven[1][:, :, 0:2], pairs(front[:]))
         for j in range(2, 4):
             nc.vector.tensor_copy(woven[0][:, :, j], planes[j][:].indirect(offs_of(0, HALF)))
-            for q in (1, 0):
+            for q in range(2):
                 lo = HALF + q * QUARTER
                 nc.scalar.activation(backs[q][:, j - 2, :], planes[j][:].indirect(offs_of(lo, lo + QUARTER)), COPY)
-        nc.scalar.copy(woven[1][:, QUARTER:HALF, 2:4], backs[1][:].rearrange("p j n -> p n j"))
-        nc.vector.tensor_copy(woven[1][:, 0:QUARTER, 2:4], backs[0][:].rearrange("p j n -> p n j"))
-
-        acts = {(b, h): keep.tile([P, HALF], F32, name="act%d_%d" % (b, h), tag="act%d_%d" % (b, h)) for b in range(2) for h in range(2)}
-        fresh = [keep.tile([P, S], F32, name="fresh%d" % b) for b in range(2)]
-        kept = keep.tile([P, S], F32, name="kept")
-        summed = keep.tile([P, S], F32, name="summed")
-        scalar_spans = ((0, HALF), (HALF, SCALAR_LOOKS_UP))
-
-        def half(tile, h):
-            return tile[:, h * HALF : (h + 1) * HALF]
-
-        def squash(b, h):
-            nc.scalar.activation(acts[(b, h)][:], banks[2 * b + h][:], TANH)
-
-        def look_up(h):
-            nc.scalar.activation(looked[h][:], mems[0][:].indirect(slot_of(*scalar_spans[h])), COPY)
-
-        def weigh(b, h):
-            nc.vector.tensor_tensor(half(fresh[b], h), acts[(b, h)][:], spread[1][h][:], MULT)
-
-        def gather_times_old(dst, b, lo, hi):
-            nc.vector.tensor_tensor(dst, mems[b][:].indirect(slot_of(lo, hi)), old_all[:, lo:hi], MULT)
-
+        nc.gpsimd.tensor_copy(woven[1][:, 0:QUARTER, 2:4], pairs(backs[0][:]))
+        nc.scalar.copy(woven[1][:, QUARTER:HALF, 2:4], pairs(backs[1][:]))
         for h in range(2):
             nc.vector.quantize_mx(out=codes[h][:].bitcast(FP8X4), scales=scales[h][:], in_=woven[h][:].rearrange("p n j -> p (n j)"))
-        for h in range(2):
-            for b in range(2):
+
+        for b in range(2):
+            for h in range(2):
                 nc.tensor.matmul_mx(
                     out=banks[2 * b + h][:],
                     lhsT=w_words[:, 2 * P * b : 2 * P * (b + 1)].bitcast(FP4X4),
@@ -133,27 +115,43 @@ def tile_picked_ema_tanh_e_kernel(tc, xT, mem, w1_words, w1_scales, old, new, of
                     stop=True,
                 )
 
-        looked = [
-            keep.tile([P, HALF], F32, name="looked0"),
-            keep.tile([P, SCALAR_LOOKS_UP - HALF], F32, name="looked1", tag="codes0", align_bytes=64),
-        ]
-        gather_times_old(kept[:, SCALAR_LOOKS_UP:S], 0, SCALAR_LOOKS_UP, S)
-        look_up(0)
-        squash(0, 0)
-        look_up(1)
-        squash(0, 1)
-        for h in range(2):
-            squash(1, h)
-        for h in range(2):
-            lo, hi = scalar_spans[h]
-            nc.vector.tensor_tensor(kept[:, lo:hi], looked[h][:], spread[0][h][:, 0 : hi - lo], MULT)
-            weigh(0, h)
-            nc.gpsimd.tensor_tensor(half(summed, h), half(kept, h), half(fresh[0], h), ADD)
+        acts = {(b, h): keep.tile([P, HALF], F32, name="act%d_%d" % (b, h), tag="act%d_%d" % (b, h)) for b in range(2) for h in range(2)}
+        fresh = [keep.tile([P, S], F32, name="fresh%d" % b) for b in range(2)]
+        looked = [keep.tile([P, S - FUSED[b]], F32, name="looked%d" % b) for b in range(2)]
+        kept_first = [keep.tile([P, HALF], F32, name="kept0_0", tag="woven0", align_bytes=64), keep.tile([P, HALF], F32, name="kept0_1", tag="codes1", align_bytes=64)]
+        summed = keep.tile([P, S], F32, name="summed")
 
+        def half(tile, h):
+            return tile[:, h * HALF : (h + 1) * HALF]
+
+        def look_up(b):
+            nc.scalar.activation(looked[b][:], mems[b][:].indirect(slot_of(FUSED[b], S)), COPY)
+
+        def gather_times_old(dst, b):
+            nc.vector.tensor_tensor(dst, mems[b][:].indirect(slot_of(0, FUSED[b])), old_first[:, 0 : FUSED[b]], MULT)
+
+        def times_old(dst, b):
+            nc.vector.tensor_tensor(dst, looked[b][:], spread[0][1][:, FUSED[b] - HALF : HALF], MULT)
+
+        def weigh(b, h):
+            nc.vector.tensor_tensor(half(fresh[b], h), acts[(b, h)][:], spread[1][h][:], MULT)
+
+        gather_times_old(kept_first[0][:], 0)
+        look_up(0)
+        for b in range(2):
+            for h in range(2):
+                nc.scalar.activation(acts[(b, h)][:], banks[2 * b + h][:], TANH)
+        look_up(1)
+        weigh(0, 0)
+        nc.gpsimd.tensor_tensor(half(summed, 0), kept_first[0][:], half(fresh[0], 0), ADD)
+        times_old(kept_first[1][:], 0)
+        weigh(0, 1)
+        nc.gpsimd.tensor_tensor(half(summed, 1), kept_first[1][:], half(fresh[0], 1), ADD)
         for h in range(2):
             weigh(1, h)
-        kept_second = keep.tile([P, S], F32, name="late", tag="act1_0")
-        gather_times_old(kept_second[:], 1, 0, S)
+        kept_second = keep.tile([P, S], F32, name="kept1", tag="act1_0")
+        gather_times_old(kept_second[:, 0 : FUSED[1]], 1)
+        times_old(kept_second[:, FUSED[1] : S], 1)
 
         for lo in range(0, S, SCATTER_PIECE):
             hi = min(lo + SCATTER_PIECE, S)

@@ -38,7 +38,7 @@ def tile_picked_ema_tanh_e_kernel(tc, xT, mem, w1_words, w1_scales, old, new, of
         slot_sb = keep.tile([P, S // 16], U16, name="slot_sb")
         planes = [keep.tile([P, T], F32, name="plane%d" % j) for j in range(4)]
         mems = [keep.tile([P, U], F32, name="mem%d" % b) for b in range(2)]
-        w_words = keep.tile([P, 2 * N], U8, name="w_words", align_bytes=64)
+        w_words = [keep.tile([P, 2 * P], U8, name="w_words%d" % b, tag="w_words%d" % b, align_bytes=64) for b in range(2)]
         w_scales = keep.tile([P, N], U8, name="w_scales", align_bytes=64)
         rows = keep.tile([P, P], F32, name="rows", tag="stage")
         cols = keep.tile([P, 2 * CHUNKS], F32, name="cols")
@@ -68,8 +68,9 @@ def tile_picked_ema_tanh_e_kernel(tc, xT, mem, w1_words, w1_scales, old, new, of
         for q in range(4):
             nc.sync.dma_start(w_scales[32 * q : 32 * q + 4, :].bitcast(I32), w1_scales[0, 4 * q : 4 * q + 4, :].bitcast(I32))
         nc.sync.dma_start(mems[0][:], mem[0:P, :])
-        nc.sync.dma_start(w_words[:].bitcast(I32), w1_words[0].bitcast(I32))
-        nc.sync.dma_start(mems[1][:], mem[P : 2 * P, :])
+        for b in range(2):
+            nc.sync.dma_start(w_words[b][:].bitcast(I32), w1_words[0, :, 2 * P * b : 2 * P * (b + 1)].bitcast(I32))
+            nc.sync.dma_start(mems[1][:, b * U // 2 : (b + 1) * U // 2], mem[P : 2 * P, b * U // 2 : (b + 1) * U // 2])
 
         old_first = keep.tile([P, FUSED[1]], F32, name="old_first")
         nc.tensor.transpose(banks[0][:, 0:P], rows[:], ident[:])
@@ -82,7 +83,8 @@ def tile_picked_ema_tanh_e_kernel(tc, xT, mem, w1_words, w1_scales, old, new, of
 
         woven = [keep.tile([P, HALF, 4], BF16, name="woven%d" % h, tag="woven%d" % h, align_bytes=64) for h in range(2)]
         front = keep.tile([P, 2, HALF], BF16, name="front", tag="stage")
-        backs = [keep.tile([P, 2, QUARTER], BF16, name="back%d" % q) for q in range(2)]
+        spans = ((0, P), (P, HALF - P), (HALF - P, HALF))
+        backs = [keep.tile([P, 2, hi - lo], BF16, name="back%d" % lo) for lo, hi in spans]
         codes = [keep.tile([P, HALF], U32, name="codes%d" % h, tag="codes%d" % h, align_bytes=64) for h in range(2)]
         scales = [keep.tile([P, HALF], U8, name="scales%d" % h, align_bytes=64) for h in range(2)]
 
@@ -93,21 +95,23 @@ def tile_picked_ema_tanh_e_kernel(tc, xT, mem, w1_words, w1_scales, old, new, of
             nc.vector.tensor_copy(woven[0][:, :, j], planes[j][:].indirect(offs_of(0, HALF)))
             nc.scalar.activation(front[:, j, :], planes[j][:].indirect(offs_of(HALF, S)), COPY)
         nc.gpsimd.tensor_copy(woven[1][:, :, 0:2], pairs(front[:]))
+        nc.vector.tensor_copy(woven[0][:, :, 2], planes[2][:].indirect(offs_of(0, HALF)))
+        for lo in (0, QUARTER):
+            nc.vector.tensor_copy(woven[0][:, lo : lo + QUARTER, 3], planes[3][:].indirect(offs_of(lo, lo + QUARTER)))
         for j in range(2, 4):
-            nc.vector.tensor_copy(woven[0][:, :, j], planes[j][:].indirect(offs_of(0, HALF)))
-            for q in range(2):
-                lo = HALF + q * QUARTER
-                nc.scalar.activation(backs[q][:, j - 2, :], planes[j][:].indirect(offs_of(lo, lo + QUARTER)), COPY)
-        nc.gpsimd.tensor_copy(woven[1][:, 0:QUARTER, 2:4], pairs(backs[0][:]))
-        nc.scalar.copy(woven[1][:, QUARTER:HALF, 2:4], pairs(backs[1][:]))
-        for h in range(2):
-            nc.vector.quantize_mx(out=codes[h][:].bitcast(FP8X4), scales=scales[h][:], in_=woven[h][:].rearrange("p n j -> p (n j)"))
+            for back, (lo, hi) in zip(backs, spans):
+                nc.scalar.activation(back[:, j - 2, :], planes[j][:].indirect(offs_of(HALF + lo, HALF + hi)), COPY)
+        for back, (lo, hi) in zip(backs[0:2], spans):
+            nc.gpsimd.tensor_copy(woven[1][:, lo:hi, 2:4], pairs(back[:]))
+        nc.scalar.copy(woven[1][:, HALF - P : HALF, 2:4], pairs(backs[2][:]))
+        for h, lo, hi in ((0, 0, QUARTER), (0, QUARTER, HALF), (1, 0, HALF)):
+            nc.vector.quantize_mx(out=codes[h][:, lo:hi].bitcast(FP8X4), scales=scales[h][:, lo:hi], in_=woven[h][:, lo:hi, :].rearrange("p n j -> p (n j)"))
 
         for b in range(2):
             for h in range(2):
                 nc.tensor.matmul_mx(
                     out=banks[2 * b + h][:],
-                    lhsT=w_words[:, 2 * P * b : 2 * P * (b + 1)].bitcast(FP4X4),
+                    lhsT=w_words[b][:].bitcast(FP4X4),
                     lhsT_scale=w_scales[:, P * b : P * (b + 1)],
                     rhs=codes[h][:].bitcast(FP8X4),
                     rhs_scale=scales[h][:],
@@ -118,8 +122,8 @@ def tile_picked_ema_tanh_e_kernel(tc, xT, mem, w1_words, w1_scales, old, new, of
         acts = {(b, h): keep.tile([P, HALF], F32, name="act%d_%d" % (b, h), tag="act%d_%d" % (b, h)) for b in range(2) for h in range(2)}
         fresh = [keep.tile([P, S], F32, name="fresh%d" % b) for b in range(2)]
         looked = [keep.tile([P, S - FUSED[b]], F32, name="looked%d" % b) for b in range(2)]
-        kept_first = [keep.tile([P, HALF], F32, name="kept0_0", tag="woven0", align_bytes=64), keep.tile([P, HALF], F32, name="kept0_1", tag="codes1", align_bytes=64)]
-        summed = keep.tile([P, S], F32, name="summed")
+        kept_first = [keep.tile([P, FUSED[0]], F32, name="kept0_0", tag="woven0", align_bytes=64), keep.tile([P, S - FUSED[0]], F32, name="kept0_1", tag="codes1", align_bytes=64)]
+        summed = keep.tile([P, S], F32, name="summed", tag="w_words1", align_bytes=64)
 
         def half(tile, h):
             return tile[:, h * HALF : (h + 1) * HALF]
@@ -143,10 +147,11 @@ def tile_picked_ema_tanh_e_kernel(tc, xT, mem, w1_words, w1_scales, old, new, of
                 nc.scalar.activation(acts[(b, h)][:], banks[2 * b + h][:], TANH)
         look_up(1)
         weigh(0, 0)
-        nc.gpsimd.tensor_tensor(half(summed, 0), kept_first[0][:], half(fresh[0], 0), ADD)
+        for lo, hi in ((0, SCATTER_PIECE), (SCATTER_PIECE, HALF)):
+            nc.gpsimd.tensor_tensor(summed[:, lo:hi], kept_first[0][:, lo:hi], fresh[0][:, lo:hi], ADD)
         times_old(kept_first[1][:], 0)
         weigh(0, 1)
-        nc.gpsimd.tensor_tensor(half(summed, 1), kept_first[1][:], half(fresh[0], 1), ADD)
+        nc.gpsimd.tensor_tensor(summed[:, FUSED[0] : S], kept_first[1][:], fresh[0][:, FUSED[0] : S], ADD)
         for h in range(2):
             weigh(1, h)
         kept_second = keep.tile([P, S], F32, name="kept1", tag="act1_0")

@@ -25,6 +25,7 @@ QUARTER = S // 4
 CHUNKS = S // P
 CLEARED = P - 2 * CHUNKS
 FUSED = (HALF, HALF + QUARTER)
+WHOLE = 192
 SCATTER_PIECE = 384
 
 
@@ -82,28 +83,24 @@ def tile_picked_ema_tanh_e_kernel(tc, xT, mem, w1_words, w1_scales, old, new, of
         nc.vector.tensor_copy(old_first[:, HALF : FUSED[1]], spread[0][1][:, 0 : FUSED[1] - HALF])
 
         woven = [keep.tile([P, HALF, 4], BF16, name="woven%d" % h, tag="woven%d" % h, align_bytes=64) for h in range(2)]
-        front = keep.tile([P, 2, HALF], BF16, name="front", tag="stage")
-        spans = ((0, P), (P, HALF - P), (HALF - P, HALF))
-        backs = [keep.tile([P, 2, hi - lo], BF16, name="back%d" % lo) for lo, hi in spans]
+        picked = keep.tile([P, 4, HALF], BF16, name="picked", tag="stage")
         codes = [keep.tile([P, HALF], U32, name="codes%d" % h, tag="codes%d" % h, align_bytes=64) for h in range(2)]
         scales = [keep.tile([P, HALF], U8, name="scales%d" % h, align_bytes=64) for h in range(2)]
 
-        def pairs(rows_of_two_planes):
-            return rows_of_two_planes.rearrange("p j n -> p n j")
+        def by_entry(rows_of_planes):
+            return rows_of_planes.rearrange("p j n -> p n j")
 
-        for j in range(2):
-            nc.vector.tensor_copy(woven[0][:, :, j], planes[j][:].indirect(offs_of(0, HALF)))
-            nc.scalar.activation(front[:, j, :], planes[j][:].indirect(offs_of(HALF, S)), COPY)
-        nc.gpsimd.tensor_copy(woven[1][:, :, 0:2], pairs(front[:]))
-        nc.vector.tensor_copy(woven[0][:, :, 2], planes[2][:].indirect(offs_of(0, HALF)))
-        for lo in (0, QUARTER):
-            nc.vector.tensor_copy(woven[0][:, lo : lo + QUARTER, 3], planes[3][:].indirect(offs_of(lo, lo + QUARTER)))
-        for j in range(2, 4):
-            for back, (lo, hi) in zip(backs, spans):
-                nc.scalar.activation(back[:, j - 2, :], planes[j][:].indirect(offs_of(HALF + lo, HALF + hi)), COPY)
-        for back, (lo, hi) in zip(backs[0:2], spans):
-            nc.gpsimd.tensor_copy(woven[1][:, lo:hi, 2:4], pairs(back[:]))
-        nc.scalar.copy(woven[1][:, HALF - P : HALF, 2:4], pairs(backs[2][:]))
+        for j in range(4):
+            for lo, hi in ((0, HALF),) if j < 3 else ((0, QUARTER), (QUARTER, HALF)):
+                nc.vector.tensor_copy(woven[0][:, lo:hi, j], planes[j][:].indirect(offs_of(lo, hi)))
+            for lo, hi in ((0, HALF),) if j < 3 else ((0, WHOLE), (QUARTER, HALF), (WHOLE, QUARTER)):
+                nc.scalar.activation(picked[:, j, lo:hi], planes[j][:].indirect(offs_of(HALF + lo, HALF + hi)), COPY)
+            if j == 1:
+                nc.gpsimd.tensor_copy(woven[1][:, QUARTER:HALF, 0:2], by_entry(picked[:, 0:2, QUARTER:HALF]))
+                nc.vector.tensor_copy(woven[1][:, WHOLE:QUARTER, 0:2], by_entry(picked[:, 0:2, WHOLE:QUARTER]))
+        nc.gpsimd.tensor_copy(woven[1][:, 0:WHOLE, :], by_entry(picked[:, :, 0:WHOLE]))
+        nc.scalar.copy(woven[1][:, QUARTER:HALF, 2:4], by_entry(picked[:, 2:4, QUARTER:HALF]))
+        nc.vector.tensor_copy(woven[1][:, WHOLE:QUARTER, 2:4], by_entry(picked[:, 2:4, WHOLE:QUARTER]))
         for h, lo, hi in ((0, 0, QUARTER), (0, QUARTER, HALF), (1, 0, HALF)):
             nc.vector.quantize_mx(out=codes[h][:, lo:hi].bitcast(FP8X4), scales=scales[h][:, lo:hi], in_=woven[h][:, lo:hi, :].rearrange("p n j -> p (n j)"))
 

@@ -24,7 +24,7 @@ HALF = S // 2
 QUARTER = S // 4
 CHUNKS = S // P
 CLEARED = P - 2 * CHUNKS
-FUSED = (HALF, HALF + QUARTER)
+FUSED = (HALF + P, HALF + QUARTER)
 WHOLE = 192
 SCATTER_PIECE = 384
 
@@ -73,7 +73,7 @@ def tile_picked_ema_tanh_e_kernel(tc, xT, mem, w1_words, w1_scales, old, new, of
             nc.sync.dma_start(w_words[b][:].bitcast(I32), w1_words[0, :, 2 * P * b : 2 * P * (b + 1)].bitcast(I32))
             nc.sync.dma_start(mems[1][:, b * U // 2 : (b + 1) * U // 2], mem[P : 2 * P, b * U // 2 : (b + 1) * U // 2])
 
-        old_first = keep.tile([P, FUSED[1]], F32, name="old_first")
+        old_first = keep.tile([P, FUSED[1]], F32, name="old_first", tag="old_first")
         nc.tensor.transpose(banks[0][:, 0:P], rows[:], ident[:])
         nc.scalar.copy(cols[:], banks[0][:, CLEARED:P])
         for c in range(2 * CHUNKS):
@@ -120,7 +120,7 @@ def tile_picked_ema_tanh_e_kernel(tc, xT, mem, w1_words, w1_scales, old, new, of
         fresh = [keep.tile([P, S], F32, name="fresh%d" % b) for b in range(2)]
         looked = [keep.tile([P, S - FUSED[b]], F32, name="looked%d" % b) for b in range(2)]
         kept_first = [keep.tile([P, FUSED[0]], F32, name="kept0_0", tag="woven0", align_bytes=64), keep.tile([P, S - FUSED[0]], F32, name="kept0_1", tag="codes1", align_bytes=64)]
-        summed = keep.tile([P, S], F32, name="summed", tag="w_words1", align_bytes=64)
+        summed = keep.tile([P, FUSED[0]], F32, name="summed", tag="w_words1", align_bytes=64)
 
         def half(tile, h):
             return tile[:, h * HALF : (h + 1) * HALF]
@@ -137,6 +137,9 @@ def tile_picked_ema_tanh_e_kernel(tc, xT, mem, w1_words, w1_scales, old, new, of
         def weigh(b, h):
             nc.vector.tensor_tensor(half(fresh[b], h), acts[(b, h)][:], spread[1][h][:], MULT)
 
+        def add(kept, lo, hi):
+            nc.gpsimd.tensor_tensor(summed[:, lo:hi], kept, fresh[0][:, lo:hi], ADD)
+
         gather_times_old(kept_first[0][:], 0)
         look_up(0)
         for b in range(2):
@@ -144,20 +147,21 @@ def tile_picked_ema_tanh_e_kernel(tc, xT, mem, w1_words, w1_scales, old, new, of
                 nc.scalar.activation(acts[(b, h)][:], banks[2 * b + h][:], TANH)
         look_up(1)
         weigh(0, 0)
-        for lo, hi in ((0, SCATTER_PIECE), (SCATTER_PIECE, HALF)):
-            nc.gpsimd.tensor_tensor(summed[:, lo:hi], kept_first[0][:, lo:hi], fresh[0][:, lo:hi], ADD)
+        add(kept_first[0][:, 0:SCATTER_PIECE], 0, SCATTER_PIECE)
         times_old(kept_first[1][:], 0)
         weigh(0, 1)
-        nc.gpsimd.tensor_tensor(summed[:, FUSED[0] : S], kept_first[1][:], fresh[0][:, FUSED[0] : S], ADD)
+        add(kept_first[0][:, SCATTER_PIECE : FUSED[0]], SCATTER_PIECE, FUSED[0])
         for h in range(2):
             weigh(1, h)
-        kept_second = keep.tile([P, S], F32, name="kept1", tag="act1_0")
+        kept_second = keep.tile([P, S], F32, name="kept1")
         gather_times_old(kept_second[:, 0 : FUSED[1]], 1)
         times_old(kept_second[:, FUSED[1] : S], 1)
+        summed_last = keep.tile([P, S - FUSED[0]], F32, name="summed_last", tag="old_first")
+        nc.vector.tensor_tensor(summed_last[:], kept_first[1][:], fresh[0][:, FUSED[0] : S], ADD)
 
-        for lo in range(0, S, SCATTER_PIECE):
-            hi = min(lo + SCATTER_PIECE, S)
+        for lo, hi in ((0, SCATTER_PIECE), (SCATTER_PIECE, FUSED[0])):
             nc.scalar.activation(mems[0][:].indirect(slot_of(lo, hi)), summed[:, lo:hi], COPY)
+        nc.scalar.activation(mems[0][:].indirect(slot_of(FUSED[0], S)), summed_last[:], COPY)
         nc.sync.dma_start(out[0:P, :], mems[0][:])
         nc.vector.tensor_tensor(mems[1][:].indirect(slot_sb[:]), kept_second[:], fresh[1][:], ADD)
         nc.sync.dma_start(out[P : 2 * P, :], mems[1][:])

@@ -24,7 +24,8 @@ HALF = S // 2
 QUARTER = S // 4
 CHUNKS = S // P
 CLEARED = P - 2 * CHUNKS
-FUSED = (HALF + P, HALF + QUARTER)
+FUSED = (HALF, HALF + P)
+ADDED = HALF + P
 WHOLE = 192
 SCATTER_PIECE = 384
 
@@ -119,8 +120,8 @@ def tile_picked_ema_tanh_e_kernel(tc, xT, mem, w1_words, w1_scales, old, new, of
         acts = {(b, h): keep.tile([P, HALF], F32, name="act%d_%d" % (b, h), tag="act%d_%d" % (b, h)) for b in range(2) for h in range(2)}
         fresh = [keep.tile([P, S], F32, name="fresh%d" % b) for b in range(2)]
         looked = [keep.tile([P, S - FUSED[b]], F32, name="looked%d" % b) for b in range(2)]
-        kept_first = [keep.tile([P, FUSED[0]], F32, name="kept0_0", tag="woven0", align_bytes=64), keep.tile([P, S - FUSED[0]], F32, name="kept0_1", tag="codes1", align_bytes=64)]
-        summed = keep.tile([P, FUSED[0]], F32, name="summed", tag="w_words1", align_bytes=64)
+        kept_first = [keep.tile([P, ADDED], F32, name="kept0_0", tag="woven0", align_bytes=64), keep.tile([P, S - ADDED], F32, name="kept0_1", tag="codes1", align_bytes=64)]
+        summed = keep.tile([P, ADDED], F32, name="summed", tag="w_words1", align_bytes=64)
 
         def half(tile, h):
             return tile[:, h * HALF : (h + 1) * HALF]
@@ -131,37 +132,39 @@ def tile_picked_ema_tanh_e_kernel(tc, xT, mem, w1_words, w1_scales, old, new, of
         def gather_times_old(dst, b):
             nc.vector.tensor_tensor(dst, mems[b][:].indirect(slot_of(0, FUSED[b])), old_first[:, 0 : FUSED[b]], MULT)
 
-        def times_old(dst, b):
-            nc.vector.tensor_tensor(dst, looked[b][:], spread[0][1][:, FUSED[b] - HALF : HALF], MULT)
+        def times_old(dst, b, lo, hi):
+            nc.vector.tensor_tensor(dst, looked[b][:, lo - FUSED[b] : hi - FUSED[b]], spread[0][1][:, lo - HALF : hi - HALF], MULT)
 
-        def weigh(b, h):
-            nc.vector.tensor_tensor(half(fresh[b], h), acts[(b, h)][:], spread[1][h][:], MULT)
+        def weigh(b, h, lo=0, hi=HALF):
+            nc.vector.tensor_tensor(half(fresh[b], h)[:, lo:hi], acts[(b, h)][:, lo:hi], spread[1][h][:, lo:hi], MULT)
 
         def add(kept, lo, hi):
             nc.gpsimd.tensor_tensor(summed[:, lo:hi], kept, fresh[0][:, lo:hi], ADD)
 
-        gather_times_old(kept_first[0][:], 0)
+        gather_times_old(kept_first[0][:, 0 : FUSED[0]], 0)
         look_up(0)
         for b in range(2):
             for h in range(2):
                 nc.scalar.activation(acts[(b, h)][:], banks[2 * b + h][:], TANH)
         look_up(1)
-        weigh(0, 0)
+        times_old(kept_first[0][:, FUSED[0] : ADDED], 0, FUSED[0], ADDED)
+        weigh(0, 0, 0, SCATTER_PIECE)
         add(kept_first[0][:, 0:SCATTER_PIECE], 0, SCATTER_PIECE)
-        times_old(kept_first[1][:], 0)
+        weigh(0, 0, SCATTER_PIECE, HALF)
+        times_old(kept_first[1][:], 0, ADDED, S)
         weigh(0, 1)
-        add(kept_first[0][:, SCATTER_PIECE : FUSED[0]], SCATTER_PIECE, FUSED[0])
+        add(kept_first[0][:, SCATTER_PIECE:ADDED], SCATTER_PIECE, ADDED)
         for h in range(2):
             weigh(1, h)
         kept_second = keep.tile([P, S], F32, name="kept1")
         gather_times_old(kept_second[:, 0 : FUSED[1]], 1)
-        times_old(kept_second[:, FUSED[1] : S], 1)
-        summed_last = keep.tile([P, S - FUSED[0]], F32, name="summed_last", tag="old_first")
-        nc.vector.tensor_tensor(summed_last[:], kept_first[1][:], fresh[0][:, FUSED[0] : S], ADD)
+        times_old(kept_second[:, FUSED[1] : S], 1, FUSED[1], S)
+        summed_last = keep.tile([P, S - ADDED], F32, name="summed_last", tag="old_first")
+        nc.vector.tensor_tensor(summed_last[:], kept_first[1][:], fresh[0][:, ADDED:S], ADD)
 
-        for lo, hi in ((0, SCATTER_PIECE), (SCATTER_PIECE, FUSED[0])):
+        for lo, hi in ((0, SCATTER_PIECE), (SCATTER_PIECE, ADDED)):
             nc.scalar.activation(mems[0][:].indirect(slot_of(lo, hi)), summed[:, lo:hi], COPY)
-        nc.scalar.activation(mems[0][:].indirect(slot_of(FUSED[0], S)), summed_last[:], COPY)
+        nc.scalar.activation(mems[0][:].indirect(slot_of(ADDED, S)), summed_last[:], COPY)
         nc.sync.dma_start(out[0:P, :], mems[0][:])
         nc.vector.tensor_tensor(mems[1][:].indirect(slot_sb[:]), kept_second[:], fresh[1][:], ADD)
         nc.sync.dma_start(out[P : 2 * P, :], mems[1][:])

@@ -24,9 +24,8 @@ HALF = S // 2
 QUARTER = S // 4
 CHUNKS = S // P
 CLEARED = P - 2 * CHUNKS
-FUSED = (HALF, HALF + P)
+FUSED = (HALF, HALF + QUARTER)
 ADDED = HALF + P
-WHOLE = 192
 SCATTER_PIECE = 384
 
 
@@ -40,7 +39,7 @@ def tile_picked_ema_tanh_e_kernel(tc, xT, mem, w1_words, w1_scales, old, new, of
         slot_sb = keep.tile([P, S // 16], U16, name="slot_sb")
         planes = [keep.tile([P, T], F32, name="plane%d" % j) for j in range(4)]
         mems = [keep.tile([P, U], F32, name="mem%d" % b) for b in range(2)]
-        w_words = [keep.tile([P, 2 * P], U8, name="w_words%d" % b, tag="w_words%d" % b, align_bytes=64) for b in range(2)]
+        w_words = [keep.tile([P, 2 * P], U8, name="w_words%d" % b, align_bytes=64) for b in range(2)]
         w_scales = keep.tile([P, N], U8, name="w_scales", align_bytes=64)
         rows = keep.tile([P, P], F32, name="rows", tag="stage")
         cols = keep.tile([P, 2 * CHUNKS], F32, name="cols")
@@ -91,17 +90,17 @@ def tile_picked_ema_tanh_e_kernel(tc, xT, mem, w1_words, w1_scales, old, new, of
         def by_entry(rows_of_planes):
             return rows_of_planes.rearrange("p j n -> p n j")
 
+        weaves = ((0, QUARTER), (QUARTER, QUARTER + P), (QUARTER + P, HALF))
         for j in range(4):
             for lo, hi in ((0, HALF),) if j < 3 else ((0, QUARTER), (QUARTER, HALF)):
                 nc.vector.tensor_copy(woven[0][:, lo:hi, j], planes[j][:].indirect(offs_of(lo, hi)))
-            for lo, hi in ((0, HALF),) if j < 3 else ((0, WHOLE), (QUARTER, HALF), (WHOLE, QUARTER)):
+            for lo, hi in ((0, HALF),) if j < 3 else weaves:
                 nc.scalar.activation(picked[:, j, lo:hi], planes[j][:].indirect(offs_of(HALF + lo, HALF + hi)), COPY)
             if j == 1:
-                nc.gpsimd.tensor_copy(woven[1][:, QUARTER:HALF, 0:2], by_entry(picked[:, 0:2, QUARTER:HALF]))
-                nc.vector.tensor_copy(woven[1][:, WHOLE:QUARTER, 0:2], by_entry(picked[:, 0:2, WHOLE:QUARTER]))
-        nc.gpsimd.tensor_copy(woven[1][:, 0:WHOLE, :], by_entry(picked[:, :, 0:WHOLE]))
-        nc.scalar.copy(woven[1][:, QUARTER:HALF, 2:4], by_entry(picked[:, 2:4, QUARTER:HALF]))
-        nc.vector.tensor_copy(woven[1][:, WHOLE:QUARTER, 2:4], by_entry(picked[:, 2:4, WHOLE:QUARTER]))
+                nc.gpsimd.tensor_copy(woven[1][:, :, 0:2], by_entry(picked[:, 0:2, :]))
+        nc.gpsimd.tensor_copy(woven[1][:, 0:QUARTER, 2:4], by_entry(picked[:, 2:4, 0:QUARTER]))
+        for lo, hi in weaves[1:]:
+            nc.scalar.copy(woven[1][:, lo:hi, 2:4], by_entry(picked[:, 2:4, lo:hi]))
         for h, lo, hi in ((0, 0, QUARTER), (0, QUARTER, HALF), (1, 0, HALF)):
             nc.vector.quantize_mx(out=codes[h][:, lo:hi].bitcast(FP8X4), scales=scales[h][:, lo:hi], in_=woven[h][:, lo:hi, :].rearrange("p n j -> p (n j)"))
 
@@ -121,7 +120,7 @@ def tile_picked_ema_tanh_e_kernel(tc, xT, mem, w1_words, w1_scales, old, new, of
         fresh = [keep.tile([P, S], F32, name="fresh%d" % b) for b in range(2)]
         looked = [keep.tile([P, S - FUSED[b]], F32, name="looked%d" % b) for b in range(2)]
         kept_first = [keep.tile([P, ADDED], F32, name="kept0_0", tag="woven0", align_bytes=64), keep.tile([P, S - ADDED], F32, name="kept0_1", tag="codes1", align_bytes=64)]
-        summed = keep.tile([P, ADDED], F32, name="summed", tag="w_words1", align_bytes=64)
+        summed = keep.tile([P, ADDED], F32, name="summed", tag="codes0", align_bytes=64)
 
         def half(tile, h):
             return tile[:, h * HALF : (h + 1) * HALF]

@@ -101,7 +101,7 @@ def tile_picked_ema_tanh_e_kernel(tc, xT, mem, w1_words, w1_scales, old, new, of
         nc.gpsimd.tensor_copy(woven[1][:, 0:QUARTER, 2:4], by_entry(picked[:, 2:4, 0:QUARTER]))
         for lo, hi in weaves[1:]:
             nc.scalar.copy(woven[1][:, lo:hi, 2:4], by_entry(picked[:, 2:4, lo:hi]))
-        for h, lo, hi in ((0, 0, QUARTER), (0, QUARTER, HALF), (1, 0, HALF)):
+        for h, lo, hi in ((0, 0, QUARTER), (0, QUARTER, HALF), (1, 0, QUARTER), (1, QUARTER, HALF)):
             nc.vector.quantize_mx(out=codes[h][:, lo:hi].bitcast(FP8X4), scales=scales[h][:, lo:hi], in_=woven[h][:, lo:hi, :].rearrange("p n j -> p (n j)"))
 
         for b in range(2):

@@ -24,9 +24,9 @@ HALF = S // 2
 QUARTER = S // 4
 CHUNKS = S // P
 CLEARED = P - 2 * CHUNKS
-FUSED = (HALF, HALF + QUARTER)
+FUSED = (HALF, S - P)
 ADDED = HALF + P
-SCATTER_PIECE = 384
+SCATTER_PIECE = 256
 
 
 def tile_picked_ema_tanh_e_kernel(tc, xT, mem, w1_words, w1_scales, old, new, offs, slot, out):

@@ -24,7 +24,7 @@ HALF = S // 2
 QUARTER = S // 4
 CHUNKS = S // P
 CLEARED = P - 2 * CHUNKS
-FUSED = (HALF, S - P)
+FUSED = (HALF + P, HALF + 192)
 ADDED = HALF + P
 SCATTER_PIECE = 256
 
@@ -71,7 +71,8 @@ def tile_picked_ema_tanh_e_kernel(tc, xT, mem, w1_words, w1_scales, old, new, of
         nc.sync.dma_start(mems[0][:], mem[0:P, :])
         for b in range(2):
             nc.sync.dma_start(w_words[b][:].bitcast(I32), w1_words[0, :, 2 * P * b : 2 * P * (b + 1)].bitcast(I32))
-            nc.sync.dma_start(mems[1][:, b * U // 2 : (b + 1) * U // 2], mem[P : 2 * P, b * U // 2 : (b + 1) * U // 2])
+            lo, hi = ((0, 3 * U // 8), (3 * U // 8, U))[b]
+            nc.sync.dma_start(mems[1][:, lo:hi], mem[P : 2 * P, lo:hi])
 
         old_first = keep.tile([P, FUSED[1]], F32, name="old_first", tag="old_first")
         nc.tensor.transpose(banks[0][:, 0:P], rows[:], ident[:])
@@ -104,17 +105,24 @@ def tile_picked_ema_tanh_e_kernel(tc, xT, mem, w1_words, w1_scales, old, new, of
         for h, lo, hi in ((0, 0, QUARTER), (0, QUARTER, HALF), (1, 0, QUARTER), (1, QUARTER, HALF)):
             nc.vector.quantize_mx(out=codes[h][:, lo:hi].bitcast(FP8X4), scales=scales[h][:, lo:hi], in_=woven[h][:, lo:hi, :].rearrange("p n j -> p (n j)"))
 
-        for b in range(2):
-            for h in range(2):
-                nc.tensor.matmul_mx(
-                    out=banks[2 * b + h][:],
-                    lhsT=w_words[b][:].bitcast(FP4X4),
-                    lhsT_scale=w_scales[:, P * b : P * (b + 1)],
-                    rhs=codes[h][:].bitcast(FP8X4),
-                    rhs_scale=scales[h][:],
-                    start=True,
-                    stop=True,
-                )
+        products = [(0, 0, 0, QUARTER), (0, 0, QUARTER, HALF), (0, 1, 0, HALF), (1, 0, 0, HALF), (1, 1, 0, HALF)]
+        sums = [banks[3][:, 0:QUARTER], banks[0][:, 0:QUARTER], banks[1][:], banks[2][:], banks[3][:]]
+
+        def multiply(i):
+            b, h, lo, hi = products[i]
+            nc.tensor.matmul_mx(
+                out=sums[i],
+                lhsT=w_words[b][:].bitcast(FP4X4),
+                lhsT_scale=w_scales[:, P * b : P * (b + 1)],
+                rhs=codes[h][:, lo:hi].bitcast(FP8X4),
+                rhs_scale=scales[h][:, lo:hi],
+                start=True,
+                stop=True,
+            )
+
+        def squash(i):
+            b, h, lo, hi = products[i]
+            nc.scalar.activation(acts[(b, h)][:, lo:hi], sums[i], TANH)
 
         acts = {(b, h): keep.tile([P, HALF], F32, name="act%d_%d" % (b, h), tag="act%d_%d" % (b, h)) for b in range(2) for h in range(2)}
         fresh = [keep.tile([P, S], F32, name="fresh%d" % b) for b in range(2)]
@@ -142,11 +150,10 @@ def tile_picked_ema_tanh_e_kernel(tc, xT, mem, w1_words, w1_scales, old, new, of
 
         gather_times_old(kept_first[0][:, 0 : FUSED[0]], 0)
         look_up(0)
-        for b in range(2):
-            for h in range(2):
-                nc.scalar.activation(acts[(b, h)][:], banks[2 * b + h][:], TANH)
+        for i in range(len(products)):
+            multiply(i)
+            squash(i)
         look_up(1)
-        times_old(kept_first[0][:, FUSED[0] : ADDED], 0, FUSED[0], ADDED)
         weigh(0, 0, 0, SCATTER_PIECE)
         add(kept_first[0][:, 0:SCATTER_PIECE], 0, SCATTER_PIECE)
         weigh(0, 0, SCATTER_PIECE, HALF)

from contextlib import ExitStack

import concourse.mybir as mybir
from concourse.masks import make_identity

K, T, S, N, U = 512, 2048, 1024, 256, 2048
FLOPS = 2 * K * S * N

F32 = mybir.dt.float32
BF16 = mybir.dt.bfloat16
I32 = mybir.dt.int32
U32 = mybir.dt.uint32
U16 = mybir.dt.uint16
U8 = mybir.dt.uint8
FP8X4 = mybir.dt.float8_e4m3fn_x4
FP4X4 = mybir.dt.float4_e2m1fn_x4
COPY = mybir.ActivationFunctionType.Copy
TANH = mybir.ActivationFunctionType.Tanh
MULT = mybir.AluOpType.mult
ADD = mybir.AluOpType.add

P = 128
HALF = S // 2
QUARTER = S // 4
CHUNKS = S // P
CLEARED = P - 2 * CHUNKS
FUSED = (HALF + P, HALF + 192)
ADDED = HALF + P
SCATTER_PIECE = 256


def tile_picked_ema_tanh_e_kernel(tc, xT, mem, w1_words, w1_scales, old, new, offs, slot, out):
    nc = tc.nc
    with ExitStack() as ctx:
        keep = ctx.enter_context(tc.tile_pool(name="keep", bufs=1))
        psum = ctx.enter_context(tc.psum_pool(name="psum", bufs=1))

        offs_sb = keep.tile([P, S // 16], U16, name="offs_sb")
        slot_sb = keep.tile([P, S // 16], U16, name="slot_sb")
        planes = [keep.tile([P, T], F32, name="plane%d" % j) for j in range(4)]
        mems = [keep.tile([P, U], F32, name="mem%d" % b) for b in range(2)]
        w_words = [keep.tile([P, 2 * P], U8, name="w_words%d" % b, align_bytes=64) for b in range(2)]
        w_scales = keep.tile([P, N], U8, name="w_scales", align_bytes=64)
        rows = keep.tile([P, P], F32, name="rows", tag="stage")
        cols = keep.tile([P, 2 * CHUNKS], F32, name="cols")
        ident = keep.tile([P, P], F32, name="ident")
        banks = [psum.tile([P, HALF], F32, name="bank%d" % i) for i in range(4)]
        spread = [[psum.tile([P, HALF], F32, name="spread%d_%d" % (i, h)) for h in range(2)] for i in range(2)]

        def offs_of(lo, hi):
            return offs_sb[:, lo // 16 : hi // 16]

        def slot_of(lo, hi):
            return slot_sb[:, lo // 16 : hi // 16]

        nc.gpsimd.memset(rows[0:CLEARED, :], 0.0)
        nc.gpsimd.memset(w_scales[:].bitcast(I32), 0)
        make_identity(nc, ident[:])
        x_rows = xT.rearrange("(p j) t -> p j t", j=4)
        for i, factor in enumerate((old, new)):
            first = CLEARED + i * CHUNKS
            nc.scalar.dma_start(rows[first : first + CHUNKS, :], factor[0:1, :].rearrange("o (c n) -> (o c) n", n=P))

        nc.sync.dma_start(planes[0][:], x_rows[:, 0, :])
        nc.sync.dma_start(offs_sb[:], offs)
        for j in range(1, 4):
            nc.sync.dma_start(planes[j][:], x_rows[:, j, :])
        nc.sync.dma_start(slot_sb[:], slot)
        for q in range(4):
            nc.sync.dma_start(w_scales[32 * q : 32 * q + 4, :].bitcast(I32), w1_scales[0, 4 * q : 4 * q + 4, :].bitcast(I32))
        nc.sync.dma_start(mems[0][:], mem[0:P, :])
        for b in range(2):
            nc.sync.dma_start(w_words[b][:].bitcast(I32), w1_words[0, :, 2 * P * b : 2 * P * (b + 1)].bitcast(I32))
            lo, hi = ((0, 3 * U // 8), (3 * U // 8, U))[b]
            nc.sync.dma_start(mems[1][:, lo:hi], mem[P : 2 * P, lo:hi])

        old_first = keep.tile([P, FUSED[1]], F32, name="old_first", tag="old_first")
        nc.tensor.transpose(banks[0][:, 0:P], rows[:], ident[:])
        nc.scalar.copy(cols[:], banks[0][:, CLEARED:P])
        for c in range(2 * CHUNKS):
            i, h, place = c // CHUNKS, c % CHUNKS // 4, c % 4
            nc.tensor.transpose(spread[i][h][:, place * P : (place + 1) * P], cols[:, c : c + 1].to_broadcast([P, P]), ident[:])
        nc.vector.tensor_copy(old_first[:, 0:HALF], spread[0][0][:])
        nc.vector.tensor_copy(old_first[:, HALF : FUSED[1]], spread[0][1][:, 0 : FUSED[1] - HALF])

        woven = [keep.tile([P, HALF, 4], BF16, name="woven%d" % h, tag="woven%d" % h, align_bytes=64) for h in range(2)]
        picked = keep.tile([P, 4, HALF], BF16, name="picked", tag="stage")
        codes = [keep.tile([P, HALF], U32, name="codes%d" % h, tag="codes%d" % h, align_bytes=64) for h in range(2)]
        scales = [keep.tile([P, HALF], U8, name="scales%d" % h, align_bytes=64) for h in range(2)]

        def by_entry(rows_of_planes):
            return rows_of_planes.rearrange("p j n -> p n j")

        weaves = ((0, QUARTER), (QUARTER, QUARTER + P), (QUARTER + P, HALF))
        for j in range(4):
            for lo, hi in ((0, HALF),) if j < 3 else ((0, QUARTER), (QUARTER, HALF)):
                nc.vector.tensor_copy(woven[0][:, lo:hi, j], planes[j][:].indirect(offs_of(lo, hi)))
            for lo, hi in ((0, HALF),) if j < 3 else weaves:
                nc.scalar.activation(picked[:, j, lo:hi], planes[j][:].indirect(offs_of(HALF + lo, HALF + hi)), COPY)
            if j == 1:
                nc.gpsimd.tensor_copy(woven[1][:, :, 0:2], by_entry(picked[:, 0:2, :]))
        nc.gpsimd.tensor_copy(woven[1][:, 0:QUARTER, 2:4], by_entry(picked[:, 2:4, 0:QUARTER]))
        for lo, hi in weaves[1:]:
            nc.scalar.copy(woven[1][:, lo:hi, 2:4], by_entry(picked[:, 2:4, lo:hi]))
        for h, lo, hi in ((0, 0, QUARTER), (0, QUARTER, HALF), (1, 0, QUARTER), (1, QUARTER, HALF)):
            nc.vector.quantize_mx(out=codes[h][:, lo:hi].bitcast(FP8X4), scales=scales[h][:, lo:hi], in_=woven[h][:, lo:hi, :].rearrange("p n j -> p (n j)"))

        products = [(0, 0, 0, QUARTER), (0, 0, QUARTER, HALF), (0, 1, 0, HALF), (1, 0, 0, HALF), (1, 1, 0, HALF)]
        sums = [banks[3][:, 0:QUARTER], banks[0][:, 0:QUARTER], banks[1][:], banks[2][:], banks[3][:]]

        def multiply(i):
            b, h, lo, hi = products[i]
            nc.tensor.matmul_mx(
                out=sums[i],
                lhsT=w_words[b][:].bitcast(FP4X4),
                lhsT_scale=w_scales[:, P * b : P * (b + 1)],
                rhs=codes[h][:, lo:hi].bitcast(FP8X4),
                rhs_scale=scales[h][:, lo:hi],
                start=True,
                stop=True,
            )

        def squash(i):
            b, h, lo, hi = products[i]
            nc.scalar.activation(acts[(b, h)][:, lo:hi], sums[i], TANH)

        acts = {(b, h): keep.tile([P, HALF], F32, name="act%d_%d" % (b, h), tag="act%d_%d" % (b, h)) for b in range(2) for h in range(2)}
        fresh = [keep.tile([P, S], F32, name="fresh%d" % b) for b in range(2)]
        looked = [keep.tile([P, S - FUSED[b]], F32, name="looked%d" % b) for b in range(2)]
        kept_first = [keep.tile([P, ADDED], F32, name="kept0_0", tag="woven0", align_bytes=64), keep.tile([P, S - ADDED], F32, name="kept0_1", tag="codes1", align_bytes=64)]
        summed = keep.tile([P, ADDED], F32, name="summed", tag="codes0", align_bytes=64)

        def half(tile, h):
            return tile[:, h * HALF : (h + 1) * HALF]

        def look_up(b):
            nc.scalar.activation(looked[b][:], mems[b][:].indirect(slot_of(FUSED[b], S)), COPY)

        def gather_times_old(dst, b):
            nc.vector.tensor_tensor(dst, mems[b][:].indirect(slot_of(0, FUSED[b])), old_first[:, 0 : FUSED[b]], MULT)

        def times_old(dst, b, lo, hi):
            nc.vector.tensor_tensor(dst, looked[b][:, lo - FUSED[b] : hi - FUSED[b]], spread[0][1][:, lo - HALF : hi - HALF], MULT)

        def weigh(b, h, lo=0, hi=HALF):
            nc.vector.tensor_tensor(half(fresh[b], h)[:, lo:hi], acts[(b, h)][:, lo:hi], spread[1][h][:, lo:hi], MULT)

        def add(kept, lo, hi):
            nc.gpsimd.tensor_tensor(summed[:, lo:hi], kept, fresh[0][:, lo:hi], ADD)

        gather_times_old(kept_first[0][:, 0 : FUSED[0]], 0)
        look_up(0)
        for i in range(len(products)):
            multiply(i)
            squash(i)
        look_up(1)
        weigh(0, 0, 0, SCATTER_PIECE)
        add(kept_first[0][:, 0:SCATTER_PIECE], 0, SCATTER_PIECE)
        weigh(0, 0, SCATTER_PIECE, HALF)
        times_old(kept_first[1][:], 0, ADDED, S)
        weigh(0, 1)
        add(kept_first[0][:, SCATTER_PIECE:ADDED], SCATTER_PIECE, ADDED)
        for h in range(2):
            weigh(1, h)
        kept_second = keep.tile([P, S], F32, name="kept1")
        gather_times_old(kept_second[:, 0 : FUSED[1]], 1)
        times_old(kept_second[:, FUSED[1] : S], 1, FUSED[1], S)
        summed_last = keep.tile([P, S - ADDED], F32, name="summed_last", tag="old_first")
        nc.vector.tensor_tensor(summed_last[:], kept_first[1][:], fresh[0][:, ADDED:S], ADD)

        for lo, hi in ((0, SCATTER_PIECE), (SCATTER_PIECE, ADDED)):
            nc.scalar.activation(mems[0][:].indirect(slot_of(lo, hi)), summed[:, lo:hi], COPY)
        nc.scalar.activation(mems[0][:].indirect(slot_of(ADDED, S)), summed_last[:], COPY)
        nc.sync.dma_start(out[0:P, :], mems[0][:])
        nc.vector.tensor_tensor(mems[1][:].indirect(slot_sb[:]), kept_second[:], fresh[1][:], ADD)
        nc.sync.dma_start(out[P : 2 * P, :], mems[1][:])
